import numpy as np
import ml_dtypes


def mxq(x, axis, fmt="e4m3"):
    dtype, down = {"e4m3": (ml_dtypes.float8_e4m3fn, 7), "e5m2": (ml_dtypes.float8_e5m2, 14)}[fmt]
    v = np.moveaxis(np.asarray(x, np.float32).astype(ml_dtypes.bfloat16).astype(np.float64), axis, -1)
    blocks = v.reshape(v.shape[:-1] + (-1, 32))
    amax = np.abs(blocks).max(-1, keepdims=True)
    byte = np.maximum(np.where(amax > 0, np.frexp(amax)[1] - 1 + 127, 0) - down, 1)
    scale = np.exp2(byte - 127.0)
    codes = (blocks / scale).astype(np.float32).astype(dtype).astype(np.float64)
    return np.moveaxis((codes * scale).reshape(v.shape), -1, axis)


WIDE = False


def mx_kscale(k):
    if not WIDE:
        return np.ones(k)
    levels = np.array([10, -10, 5, -5, 0])
    if k % 512:
        return np.exp2(np.random.permutation(np.resize(levels, k // 32))).repeat(32)
    a = np.empty((k // 512, 16))
    for p in range(k // 512):
        a[p, :8] = np.random.permutation(np.resize(levels, 8))
        for g in range(8):
            far = levels[np.abs(levels - a[p, g]) >= 10]
            a[p, g + 8] = far[np.random.randint(len(far))]
    return np.exp2(a.ravel()).repeat(32)


def f64(x):
    return np.asarray(x).astype(np.float64)


def striped(idx):
    return np.tile(idx.reshape(-1, 16).T, (8, 1)).astype(np.uint16)


def unstriped(offs):
    return offs[:16].T.reshape(-1).astype(np.int64)


def striped8(idx):
    return np.concatenate([x.reshape(-1, 16).T for x in idx]).astype(np.uint16)


def runs(offs, k):
    lists = np.stack([offs[16 * r : 16 * r + 16].T.reshape(-1) for r in range(8)]).astype(np.int64)
    return lists[np.arange(k) % 512 // 64]


def pack_weight(w):
    k, n = w.shape
    w = f64(np.asarray(w, np.float32).astype(ml_dtypes.bfloat16)).reshape(k // 32, 32, n)
    amax = np.abs(w).max(1)
    byte = np.clip(np.where(amax > 0, np.frexp(amax)[1] - 1 + 127 - 7, 1), 1, 254)
    scaled = (w * np.exp2(127.0 - byte)[:, None, :]).reshape(k, n).astype(np.float32)
    words = np.ascontiguousarray(scaled.reshape(k // 512, 128, 4, n).transpose(0, 1, 3, 2)).astype(ml_dtypes.float8_e4m3fn).view(np.uint8)
    return words, np.ascontiguousarray(byte.astype(np.uint8).reshape(k // 512, 16, n))


def unpack_weight(words, scales):
    g, p, n, _ = words.shape
    vals = np.ascontiguousarray(words).view(ml_dtypes.float8_e4m3fn).astype(np.float64) * np.repeat(np.exp2(scales.astype(np.float64) - 127.0), 8, axis=1)[..., None]
    return vals.transpose(0, 1, 3, 2).reshape(g * 512, n)


def sigmoid(v):
    return 1.0 / (1.0 + np.exp(-np.maximum(v, -700.0)))


K, T, S, V, N, H = 1024, 2048, 512, 256, 512, 512


def setup_inputs():
    n = np.random.standard_normal
    s = mx_kscale(K)[:, None]
    u = mx_kscale(H)
    packed_xT = pack_weight(n((K, T)) * s)
    return {
        "x_words": packed_xT[0],
        "x_scales": packed_xT[1],
        "w1": (n((K, H)) / np.sqrt(K) / s).astype(np.float32),
        "w2": (n((K, H)) / np.sqrt(K) / s * u).astype(np.float32),
        "pose": n((H, V)).astype(np.float32),
        "lg1": n((H, V)).astype(np.float32),
        "lg2": n((H, V)).astype(np.float32),
        "w3": (n((H, N)) / np.sqrt(H) / u[:, None]).astype(np.float32),
        "offs": striped(np.random.permutation(T)[:S]),
        "p1": striped8(np.stack([np.random.permutation(S)[:V] for _ in range(8)])),
        "p2": striped8(np.stack([np.random.permutation(S)[:V] for _ in range(8)])),
    }


def reference(x_words, x_scales, w1, w2, pose, lg1, lg2, w3, offs, p1, p2):
    xq = unpack_weight(x_words, x_scales)[:, unstriped(offs)]
    e = mxq(f64(w1), 0, "e4m3").T @ xq
    val = mxq(f64(w2), 0, "e4m3").T @ xq
    z = (sigmoid(f64(lg1) + f64(pose) * (e[np.arange(H)[:, None], runs(p1, H)]))) * (val[np.arange(H)[:, None], runs(p1, H)]) + (sigmoid(f64(lg2) + f64(pose) * (e[np.arange(H)[:, None], runs(p2, H)]))) * (val[np.arange(H)[:, None], runs(p2, H)])
    return mxq(f64(w3), 0, "e4m3").T @ mxq(z, 0, "e4m3")

@@ -1,0 +1,257 @@
+from contextlib import ExitStack
+
+import concourse.mybir as mybir
+
+K, T, S, V, N, H = 1024, 2048, 512, 256, 512, 512
+FLOPS = 2 * (2 * K * H * S + H * N * V)
+
+F32 = mybir.dt.float32
+BF16 = mybir.dt.bfloat16
+I32 = mybir.dt.int32
+U32 = mybir.dt.uint32
+U16 = mybir.dt.uint16
+U8 = mybir.dt.uint8
+FP8X4 = mybir.dt.float8_e4m3fn_x4
+MULT = mybir.AluOpType.mult
+ADD = mybir.AluOpType.add
+SIGMOID = mybir.ActivationFunctionType.Sigmoid
+
+P = 128
+PACK = 4
+K_PASS = P * PACK
+PASSES = K // K_PASS
+HALF = V // 2
+
+
+def tile_picked_agree_none_p_kernel(
+    tc, x_words, x_scales, w1, w2, pose, lg1, lg2, w3, offs, p1, p2, out
+):
+    nc = tc.nc
+    with ExitStack() as ctx:
+        keep = ctx.enter_context(tc.tile_pool(name="keep", bufs=1))
+        psum = ctx.enter_context(tc.psum_pool(name="psum", bufs=1))
+
+        def sb(name, shape, dtype):
+            return keep.tile(shape, dtype, name=name, align_bytes=64)
+
+        offs_sb = sb("offs_sb", [P, S // 16], U16)
+        lists = [sb("p1_sb", [P, V // 16], U16), sb("p2_sb", [P, V // 16], U16)]
+        xs_all = sb("xs_all", [P, T], U8)
+        xw_all = [sb(f"xw_all{z}", [P, T], U32) for z in range(PASSES)]
+        xs = sb("xs", [P, S], U8)
+        xw = [sb(f"xw{z}", [P, S], U32) for z in range(PASSES)]
+        raw = {(w, z): sb(f"raw{w}{z}", [P, PACK, H], F32) for w in range(2) for z in range(PASSES)}
+        raw3 = sb("raw3", [P, PACK, N], F32)
+        pose_sb = [sb(f"pose{a}", [P, 2, V], F32) for a in range(2)]
+        lg_sb = [sb(f"lg{a}", [P, 2, 2, V], F32) for a in range(2)]
+
+        def load_rows(dst, src, z):
+            nc.sync.dma_start(out=dst[:], in_=src[z * K_PASS : (z + 1) * K_PASS, :].rearrange("(p j) c -> p j c", j=PACK))
+
+        def load_words(z):
+            nc.sync.dma_start(
+                out=xw_all[z][:].bitcast(I32), in_=x_words[z].rearrange("p n r -> p (n r)").bitcast(I32)
+            )
+
+        def load_pair(dst, src, a):
+            nc.sync.dma_start(out=dst, in_=src.rearrange("(p t) v -> p t v", t=PACK)[:, 2 * a : 2 * a + 2, :])
+
+        nc.vector.memset(xs_all[:].bitcast(I32), 0)
+        load_rows(raw[0, 0], w1, 0)
+        for q in range(4):
+            nc.sync.dma_start(
+                out=xs_all[32 * q : 32 * q + 4 * PASSES, :].bitcast(I32),
+                in_=x_scales[:, 4 * q : 4 * q + 4, :].bitcast(I32),
+            )
+        nc.sync.dma_start(offs_sb[:], offs)
+        load_words(0)
+        load_rows(raw[0, 1], w1, 1)
+        load_words(1)
+        nc.sync.dma_start(lists[0][:], p1)
+        load_pair(pose_sb[0][:], pose, 0)
+        nc.sync.dma_start(lists[1][:], p2)
+        load_rows(raw[1, 0], w2, 0)
+        load_pair(pose_sb[1][:], pose, 1)
+        load_rows(raw[1, 1], w2, 1)
+        for a in range(2):
+            load_pair(lg_sb[a][:, 0], lg1, a)
+            load_pair(lg_sb[a][:, 1], lg2, a)
+        load_rows(raw3, w3, 0)
+
+        grouped, codes, scales = {}, {}, {}
+
+        def copy_on(engine, out_ap, in_ap):
+            if engine == "vector":
+                nc.vector.tensor_copy(out=out_ap, in_=in_ap)
+            else:
+                nc.scalar.copy(out=out_ap, in_=in_ap)
+
+        def cast(w, z, a, engine):
+            g = sb(f"grp{w}{z}{a}", [P, 2, P, PACK], BF16)
+            grouped[w, z, a] = g
+            src = raw[w, z][:].rearrange("p j (m a b) -> p a m j b", a=2, b=2)[:, a]
+            copy_on(engine, g[:].rearrange("p b m j -> p m j b"), src)
+
+        def quant(key, width):
+            name = "".join(str(x) for x in key)
+            codes[key] = sb(f"codes{name}", [P, width], U32)
+            scales[key] = sb(f"scales{name}", [P, width], U8)
+            g = grouped[key]
+            flat = g[:].rearrange("p b m j -> p (b m j)")
+            nc.vector.quantize_mx(out=codes[key][:].bitcast(FP8X4), scales=scales[key][:], in_=flat)
+
+        banks = {}
+
+        bank_of = {(0, 0, 0): 0, (0, 0, S // 2): 1, (0, 1, 0): 2, (0, 2, 0): 3, (0, 3, 0): 4,
+                   (1, 0, 0): 5, (1, 1, 0): 6, (1, 2, 0): 7, (1, 3, 0): 0}
+
+        def first_mm(w, z, t, lo=0, hi=S):
+            if z == 0:
+                banks[w, t, lo] = psum.tile([P, hi - lo], F32, name=f"acc{w}{t}{lo}", tag=f"bank{bank_of[w, t, lo]}")
+            key, cols = (w, z, t // 2), slice(P * (t % 2), P * (t % 2 + 1))
+            nc.tensor.matmul_mx(
+                out=banks[w, t, lo][:],
+                lhsT=codes[key][:, cols].bitcast(FP8X4),
+                lhsT_scale=scales[key][:, cols],
+                rhs=xw[z][:, lo:hi].bitcast(FP8X4),
+                rhs_scale=xs[4 * z : P, lo:hi],
+                start=(z == 0),
+                stop=(z == PASSES - 1),
+            )
+
+        rows = {(w, t): sb(f"rows{w}{t}", [P, S], F32) for w in range(2) for t in range(PACK)}
+
+        def evac(w, t, lo=0, hi=S):
+            nc.scalar.copy(out=rows[w, t][:, lo:hi], in_=banks[w, t, lo][:])
+
+        agree = [sb(f"agree{a}", [P, 2, 2, V], F32) for a in range(2)]
+        gate = [sb(f"gate{t}", [P, 2, V], F32) for t in range(PACK)]
+        votes = sb("votes", [P, 2, PACK, V], F32)
+
+        def gather_keys(t):
+            for l in range(2):
+                nc.vector.tensor_tensor(
+                    agree[t // 2][:, l, t % 2, :], rows[0, t][:].indirect(lists[l][:]), pose_sb[t // 2][:, t % 2, :], MULT
+                )
+
+        def add_logits(a):
+            nc.vector.tensor_tensor(agree[a][:], agree[a][:], lg_sb[a][:], ADD)
+
+        def sigmoid(t):
+            nc.scalar.activation(out=gate[t][:], in_=agree[t // 2][:, :, t % 2, :], func=SIGMOID)
+
+        def gather_votes(t, lo, hi):
+            for l in range(2):
+                nc.vector.tensor_tensor(
+                    votes[:, l, t, lo:hi],
+                    rows[1, t][:].indirect(lists[l][:, lo // 16 : hi // 16]),
+                    gate[t][:, l, lo:hi],
+                    MULT,
+                )
+
+        def sum_votes(h):
+            g = sb(f"zgrp{h}", [P, 1, HALF, PACK], BF16)
+            grouped["z", h] = g
+            walk = "p t (c i) -> p c t i"
+            nc.vector.tensor_tensor(
+                g[:, 0].rearrange("p (c i) t -> p c t i", i=2),
+                votes[:, 0, :, h * HALF : (h + 1) * HALF].rearrange(walk, i=2),
+                votes[:, 1, :, h * HALF : (h + 1) * HALF].rearrange(walk, i=2),
+                ADD,
+            )
+
+        def cast3(a):
+            g = sb(f"grp3{a}", [P, 1, N // 2, PACK], BF16)
+            grouped["w3", a] = g
+            src = raw3[:, :, a * N // 2 : (a + 1) * N // 2].rearrange("p j (c i) -> p c j i", i=2)
+            nc.scalar.copy(out=g[:, 0].rearrange("p (c i) j -> p c j i", i=2), in_=src)
+
+        def last_layer(h, engines):
+            for a in range(2):
+                acc = psum.tile([P, 2, HALF], F32, name=f"out{h}{a}", tag=f"bank{1 + 2 * h + a}")
+                for b in range(2):
+                    cols = slice(P * b, P * (b + 1))
+                    nc.tensor.matmul_mx(
+                        out=acc[:, b, :],
+                        lhsT=codes["w3", a][:, cols].bitcast(FP8X4),
+                        lhsT_scale=scales["w3", a][:, cols],
+                        rhs=codes["z", h][:].bitcast(FP8X4),
+                        rhs_scale=scales["z", h][:],
+                        start=True,
+                        stop=True,
+                    )
+                res = sb(f"res{h}{a}", [P, 2, HALF], F32)
+                copy_on(engines[a], res[:], acc[:])
+                dst = out.rearrange("(a b p) v -> a p b v", a=2, b=2)[a, :, :, h * HALF : (h + 1) * HALF]
+                nc.sync.dma_start(out=dst, in_=res[:])
+
+        cast(0, 0, 0, "scalar")
+        cast(0, 0, 1, "scalar")
+        quant((0, 0, 0), 2 * P)
+        nc.vector.tensor_copy(xs[:], xs_all[:].indirect(offs_sb[:]))
+        nc.vector.tensor_copy(xw[0][:], xw_all[0][:].indirect(offs_sb[:]))
+        quant((0, 0, 1), 2 * P)
+        first_mm(0, 0, 0, 0, S // 2)
+        first_mm(0, 0, 0, S // 2, S)
+        for t in range(1, PACK):
+            first_mm(0, 0, t)
+        cast(0, 1, 0, "vector")
+        cast(0, 1, 1, "scalar")
+        quant((0, 1, 0), 2 * P)
+        quant((0, 1, 1), 2 * P)
+        for lo in (0, S // 2):
+            hi = lo + S // 2
+            nc.vector.tensor_copy(xw[1][:, lo:hi], xw_all[1][:].indirect(offs_sb[:, lo // 16 : hi // 16]))
+            first_mm(0, 1, 0, lo, hi)
+            evac(0, 0, lo, hi)
+        for t in range(1, PACK):
+            first_mm(0, 1, t)
+        evac(0, 1)
+        gather_keys(0)
+        evac(0, 2)
+        cast(1, 0, 0, "scalar")
+        gather_keys(1)
+        evac(0, 3)
+        cast(1, 0, 1, "scalar")
+        quant((1, 0, 0), 2 * P)
+        first_mm(1, 0, 0)
+        first_mm(1, 0, 1)
+        gather_keys(2)
+        cast(1, 1, 0, "scalar")
+        quant((1, 0, 1), 2 * P)
+        first_mm(1, 0, 2)
+        first_mm(1, 0, 3)
+        quant((1, 1, 0), 2 * P)
+        first_mm(1, 1, 0)
+        first_mm(1, 1, 1)
+        cast(1, 1, 1, "scalar")
+        evac(1, 0)
+        gather_keys(3)
+        quant((1, 1, 1), 2 * P)
+        first_mm(1, 1, 2)
+        first_mm(1, 1, 3)
+        add_logits(0)
+        sigmoid(0)
+        evac(1, 1)
+        sigmoid(1)
+        add_logits(1)
+        evac(1, 2)
+        sigmoid(2)
+        evac(1, 3)
+        sigmoid(3)
+        cast3(0)
+        cast3(1)
+        for t in range(2):
+            gather_votes(t, 0, V)
+        quant(("w3", 0), N // 2)
+        quant(("w3", 1), N // 2)
+        gather_votes(2, 0, HALF)
+        gather_votes(3, 0, HALF)
+        sum_votes(0)
+        gather_votes(2, HALF, V)
+        quant(("z", 0), HALF)
+        last_layer(0, ("scalar", "scalar"))
+        gather_votes(3, HALF, V)
+        sum_votes(1)
+        quant(("z", 1), HALF)
+        last_layer(1, ("scalar", "vector"))

@@ -44,6 +44,7 @@ def tile_picked_agree_none_p_kernel(
         raw3 = sb("raw3", [P, PACK, N], F32)
         pose_sb = [sb(f"pose{a}", [P, 2, V], F32) for a in range(2)]
         lg_sb = [sb(f"lg{a}", [P, 2, 2, V], F32) for a in range(2)]
+        warm = sb("warm", [P, 1], F32)
 
         def load_rows(dst, src, z):
             nc.sync.dma_start(out=dst[:], in_=src[z * K_PASS : (z + 1) * K_PASS, :].rearrange("(p j) c -> p j c", j=PACK))
@@ -57,6 +58,8 @@ def tile_picked_agree_none_p_kernel(
             nc.sync.dma_start(out=dst, in_=src.rearrange("(p t) v -> p t v", t=PACK)[:, 2 * a : 2 * a + 2, :])
 
         nc.vector.memset(xs_all[:].bitcast(I32), 0)
+        nc.vector.memset(warm[:], 0.0)
+        nc.scalar.activation(out=warm[:], in_=warm[:], func=SIGMOID)
         load_rows(raw[0, 0], w1, 0)
         for q in range(4):
             nc.sync.dma_start(

@@ -21,6 +21,7 @@ PACK = 4
 K_PASS = P * PACK
 PASSES = K // K_PASS
 HALF = V // 2
+W3_PIECES = ((0, 256), (256, 384), (384, 512))
 
 
 def tile_picked_agree_none_p_kernel(
@@ -152,41 +153,52 @@ def tile_picked_agree_none_p_kernel(
                     MULT,
                 )
 
+        z_grouped = sb("z_grouped", [P, V, PACK], BF16)
+        z_codes = sb("z_codes", [P, V], U32)
+        z_scales = sb("z_scales", [P, V], U8)
+
         def sum_votes(h):
-            g = sb(f"zgrp{h}", [P, 1, HALF, PACK], BF16)
-            grouped["z", h] = g
+            cols = slice(h * HALF, (h + 1) * HALF)
             walk = "p t (c i) -> p c t i"
             nc.vector.tensor_tensor(
-                g[:, 0].rearrange("p (c i) t -> p c t i", i=2),
-                votes[:, 0, :, h * HALF : (h + 1) * HALF].rearrange(walk, i=2),
-                votes[:, 1, :, h * HALF : (h + 1) * HALF].rearrange(walk, i=2),
+                z_grouped[:, cols, :].rearrange("p (c i) t -> p c t i", i=2),
+                votes[:, 0, :, cols].rearrange(walk, i=2),
+                votes[:, 1, :, cols].rearrange(walk, i=2),
                 ADD,
             )
 
-        def cast3(a):
-            g = sb(f"grp3{a}", [P, 1, N // 2, PACK], BF16)
-            grouped["w3", a] = g
-            src = raw3[:, :, a * N // 2 : (a + 1) * N // 2].rearrange("p j (c i) -> p c j i", i=2)
+        def quant_z(h):
+            cols = slice(h * HALF, (h + 1) * HALF)
+            nc.vector.quantize_mx(
+                out=z_codes[:, cols].bitcast(FP8X4),
+                scales=z_scales[:, cols],
+                in_=z_grouped[:, cols, :].rearrange("p v t -> p (v t)"),
+            )
+
+        def cast3(lo, hi):
+            g = sb(f"grp3{lo}", [P, 1, hi - lo, PACK], BF16)
+            grouped["w3", lo] = g
+            src = raw3[:, :, lo:hi].rearrange("p j (c i) -> p c j i", i=2)
             nc.scalar.copy(out=g[:, 0].rearrange("p (c i) j -> p c j i", i=2), in_=src)
 
-        def last_layer(h, engines):
-            for a in range(2):
-                acc = psum.tile([P, 2, HALF], F32, name=f"out{h}{a}", tag=f"bank{1 + 2 * h + a}")
-                for b in range(2):
-                    cols = slice(P * b, P * (b + 1))
-                    nc.tensor.matmul_mx(
-                        out=acc[:, b, :],
-                        lhsT=codes["w3", a][:, cols].bitcast(FP8X4),
-                        lhsT_scale=scales["w3", a][:, cols],
-                        rhs=codes["z", h][:].bitcast(FP8X4),
-                        rhs_scale=scales["z", h][:],
-                        start=True,
-                        stop=True,
-                    )
-                res = sb(f"res{h}{a}", [P, 2, HALF], F32)
-                copy_on(engines[a], res[:], acc[:])
-                dst = out.rearrange("(a b p) v -> a p b v", a=2, b=2)[a, :, :, h * HALF : (h + 1) * HALF]
-                nc.sync.dma_start(out=dst, in_=res[:])
+        def last_layer(lo, hi):
+            quant(("w3", lo), hi - lo)
+            for m0 in range(lo, hi, P):
+                block = m0 // P
+                cols = slice(m0 - lo, m0 - lo + P)
+                acc = psum.tile([P, V], F32, name=f"out{block}", tag=f"bank{1 + block}")
+                nc.tensor.matmul_mx(
+                    out=acc[:],
+                    lhsT=codes["w3", lo][:, cols].bitcast(FP8X4),
+                    lhsT_scale=scales["w3", lo][:, cols],
+                    rhs=z_codes[:].bitcast(FP8X4),
+                    rhs_scale=z_scales[:],
+                    start=True,
+                    stop=True,
+                )
+                res = sb(f"res{block}", [P, V], F32)
+                copy_on("vector" if block % 2 else "scalar", res[:], acc[:])
+                nc.sync.dma_start(out=out[m0 : m0 + P, :], in_=res[:])
 
         cast(0, 0, 0, "scalar")
         cast(0, 0, 1, "scalar")
@@ -242,19 +254,15 @@ def tile_picked_agree_none_p_kernel(
         sigmoid(2)
         evac(1, 3)
         sigmoid(3)
-        cast3(0)
-        cast3(1)
-        for t in range(2):
+        for lo, hi in W3_PIECES:
+            cast3(lo, hi)
+        for t in range(PACK - 1):
             gather_votes(t, 0, V)
-        quant(("w3", 0), N // 2)
-        quant(("w3", 1), N // 2)
-        gather_votes(2, 0, HALF)
-        gather_votes(3, 0, HALF)
-        sum_votes(0)
-        gather_votes(2, HALF, V)
-        quant(("z", 0), HALF)
-        last_layer(0, ("scalar", "scalar"))
-        gather_votes(3, HALF, V)
-        sum_votes(1)
-        quant(("z", 1), HALF)
-        last_layer(1, ("scalar", "vector"))
+        for h in range(2):
+            gather_votes(PACK - 1, h * HALF, (h + 1) * HALF)
+        for h in range(2):
+            sum_votes(h)
+        for h in range(2):
+            quant_z(h)
+        for lo, hi in W3_PIECES:
+            last_layer(lo, hi)

@@ -41,7 +41,8 @@ def tile_picked_agree_none_p_kernel(
         xw_all = [sb(f"xw_all{z}", [P, T], U32) for z in range(PASSES)]
         xs = sb("xs", [P, S], U8)
         xw = [sb(f"xw{z}", [P, S], U32) for z in range(PASSES)]
-        raw = {(w, z): sb(f"raw{w}{z}", [P, PACK, H], F32) for w in range(2) for z in range(PASSES)}
+        raw = {(w, z): sb(f"raw{w}{z}", [P, PACK, H], F32) for w in range(2) for z in range(PASSES) if (w, z) != (0, 1)}
+        late = [sb(f"late{h}", [P, 2, H], F32) for h in range(2)]
         raw3 = sb("raw3", [P, PACK, N], F32)
         pose_sb = [sb(f"pose{a}", [P, 2, V], F32) for a in range(2)]
         lg_sb = [sb(f"lg{a}", [P, 2, 2, V], F32) for a in range(2)]
@@ -58,19 +59,27 @@ def tile_picked_agree_none_p_kernel(
         def load_pair(dst, src, a):
             nc.sync.dma_start(out=dst, in_=src.rearrange("(p t) v -> p t v", t=PACK)[:, 2 * a : 2 * a + 2, :])
 
-        nc.vector.memset(xs_all[:].bitcast(I32), 0)
+        nc.gpsimd.memset(xs_all[:].bitcast(I32), 0)
         nc.vector.memset(warm[:], 0.0)
         nc.scalar.activation(out=warm[:], in_=warm[:], func=SIGMOID)
         load_rows(raw[0, 0], w1, 0)
-        for q in range(4):
-            nc.sync.dma_start(
-                out=xs_all[32 * q : 32 * q + 4 * PASSES, :].bitcast(I32),
-                in_=x_scales[:, 4 * q : 4 * q + 4, :].bitcast(I32),
-            )
+        def load_scales(z):
+            for q in range(4):
+                nc.sync.dma_start(
+                    out=xs_all[32 * q + 4 * z : 32 * q + 4 * z + 4, :].bitcast(I32),
+                    in_=x_scales[z, 4 * q : 4 * q + 4, :].bitcast(I32),
+                )
+
+        load_scales(0)
         nc.sync.dma_start(offs_sb[:], offs)
         load_words(0)
-        load_rows(raw[0, 1], w1, 1)
+        load_scales(1)
         load_words(1)
+        for h in range(2):
+            nc.sync.dma_start(
+                out=late[h][:],
+                in_=w1[K_PASS:, :].rearrange("(p j) c -> p j c", j=PACK)[:, 2 * h : 2 * h + 2, :],
+            )
         nc.sync.dma_start(lists[0][:], p1)
         load_pair(pose_sb[0][:], pose, 0)
         nc.sync.dma_start(lists[1][:], p2)
@@ -103,6 +112,25 @@ def tile_picked_agree_none_p_kernel(
             g = grouped[key]
             flat = g[:].rearrange("p b m j -> p (b m j)")
             nc.vector.quantize_mx(out=codes[key][:].bitcast(FP8X4), scales=scales[key][:], in_=flat)
+
+        for a in range(2):
+            grouped[0, 1, a] = sb(f"grp01{a}", [P, 2, P, PACK], BF16)
+            codes[0, 1, a] = sb(f"codes01{a}", [P, 2 * P], U32)
+            scales[0, 1, a] = sb(f"scales01{a}", [P, 2 * P], U8)
+
+        def late_cast(h, a, engine, lo, hi):
+            src = late[h][:].rearrange("p j (m a b) -> p a m j b", a=2, b=2)[:, a, lo:hi]
+            dst = grouped[0, 1, a][:, :, lo:hi, 2 * h : 2 * h + 2]
+            copy_on(engine, dst.rearrange("p b m j -> p m j b"), src)
+
+        def late_quant(t):
+            key, b = (0, 1, t // 2), t % 2
+            cols = slice(b * P, (b + 1) * P)
+            nc.vector.quantize_mx(
+                out=codes[key][:, cols].bitcast(FP8X4),
+                scales=scales[key][:, cols],
+                in_=grouped[key][:, b].rearrange("p m j -> p (m j)"),
+            )
 
         banks = {}
 
@@ -210,15 +238,18 @@ def tile_picked_agree_none_p_kernel(
         first_mm(0, 0, 0, S // 2, S)
         for t in range(1, PACK):
             first_mm(0, 0, t)
-        cast(0, 1, 0, "vector")
-        cast(0, 1, 1, "scalar")
-        quant((0, 1, 0), 2 * P)
-        quant((0, 1, 1), 2 * P)
+        nc.vector.tensor_copy(xw[1][:], xw_all[1][:].indirect(offs_sb[:]))
+        late_cast(0, 0, "vector", 0, P)
+        late_cast(0, 1, "scalar", 0, P)
+        for a in range(2):
+            late_cast(1, a, "vector", 0, P // 2)
+            late_cast(1, a, "scalar", P // 2, P)
+        late_quant(0)
         for lo in (0, S // 2):
-            hi = lo + S // 2
-            nc.vector.tensor_copy(xw[1][:, lo:hi], xw_all[1][:].indirect(offs_sb[:, lo // 16 : hi // 16]))
-            first_mm(0, 1, 0, lo, hi)
-            evac(0, 0, lo, hi)
+            first_mm(0, 1, 0, lo, lo + S // 2)
+            evac(0, 0, lo, lo + S // 2)
+        for t in range(1, PACK):
+            late_quant(t)
         for t in range(1, PACK):
             first_mm(0, 1, t)
         evac(0, 1)

@@ -32,8 +32,8 @@ def tile_picked_agree_none_p_kernel(
         keep = ctx.enter_context(tc.tile_pool(name="keep", bufs=1))
         psum = ctx.enter_context(tc.psum_pool(name="psum", bufs=1))
 
-        def sb(name, shape, dtype):
-            return keep.tile(shape, dtype, name=name, align_bytes=64)
+        def sb(name, shape, dtype, tag=None):
+            return keep.tile(shape, dtype, name=name, tag=tag or name, align_bytes=64)
 
         offs_sb = sb("offs_sb", [P, S // 16], U16)
         lists = [sb("p1_sb", [P, V // 16], U16), sb("p2_sb", [P, V // 16], U16)]
@@ -156,21 +156,31 @@ def tile_picked_agree_none_p_kernel(
         def evac(w, t, lo=0, hi=S):
             nc.scalar.copy(out=rows[w, t][:, lo:hi], in_=banks[w, t, lo][:])
 
-        agree = [sb(f"agree{a}", [P, 2, 2, V], F32) for a in range(2)]
+        agree01 = sb("agree01", [P, 2, 2, V], F32)
+        agree23 = sb("agree23", [P, 2, 2, V], F32)
+        agree = {(t, l): (agree01, agree23)[t // 2][:, l, t % 2, :] for t in range(PACK) for l in range(2)}
         gate = [sb(f"gate{t}", [P, 2, V], F32) for t in range(PACK)]
         votes = sb("votes", [P, 2, PACK, V], F32)
 
         def gather_keys(t):
             for l in range(2):
+                if (t, l) == (3, 1):
+                    agree[t, l] = sb("agree_last", [P, V], F32, "grp110")[:]
                 nc.vector.tensor_tensor(
-                    agree[t // 2][:, l, t % 2, :], rows[0, t][:].indirect(lists[l][:]), pose_sb[t // 2][:, t % 2, :], MULT
+                    agree[t, l], rows[0, t][:].indirect(lists[l][:]), pose_sb[t // 2][:, t % 2, :], MULT
                 )
 
         def add_logits(a):
-            nc.vector.tensor_tensor(agree[a][:], agree[a][:], lg_sb[a][:], ADD)
+            if a == 0:
+                nc.vector.tensor_tensor(agree01[:], agree01[:], lg_sb[0][:], ADD)
+            else:
+                flat = "p l t v -> p (l t v)"
+                first = agree23[:].rearrange(flat)[:, : 3 * V]
+                nc.vector.tensor_tensor(first, first, lg_sb[1][:].rearrange(flat)[:, : 3 * V], ADD)
+                nc.vector.tensor_tensor(agree23[:, 1, 1, :], agree[3, 1], lg_sb[1][:, 1, 1, :], ADD)
 
         def sigmoid(t):
-            nc.scalar.activation(out=gate[t][:], in_=agree[t // 2][:, :, t % 2, :], func=SIGMOID)
+            nc.scalar.activation(out=gate[t][:], in_=(agree01, agree23)[t // 2][:, :, t % 2, :], func=SIGMOID)
 
         def gather_votes(t, lo, hi):
             for l in range(2):

@@ -63,12 +63,13 @@ def tile_picked_agree_none_p_kernel(
         nc.vector.memset(warm[:], 0.0)
         nc.scalar.activation(out=warm[:], in_=warm[:], func=SIGMOID)
         load_rows(raw[0, 0], w1, 0)
-        def load_scales(z):
-            for q in range(4):
-                nc.sync.dma_start(
-                    out=xs_all[32 * q + 4 * z : 32 * q + 4 * z + 4, :].bitcast(I32),
-                    in_=x_scales[z, 4 * q : 4 * q + 4, :].bitcast(I32),
-                )
+        def load_scales(h):
+            for r in (2 * h, 2 * h + 1):
+                for z in range(PASSES):
+                    nc.sync.dma_start(
+                        out=xs_all[4 * z + r : P : 32, :].bitcast(I32),
+                        in_=x_scales[z, r : 16 : 4, :].bitcast(I32),
+                    )
 
         load_scales(0)
         nc.sync.dma_start(offs_sb[:], offs)

@@ -44,17 +44,22 @@ def tile_picked_agree_none_p_kernel(
         raw = {(w, z): sb(f"raw{w}{z}", [P, PACK, H], F32) for w in range(2) for z in range(PASSES) if (w, z) != (0, 1)}
         late = [sb(f"late{h}", [P, 2, H], F32) for h in range(2)]
         raw3 = sb("raw3", [P, PACK, N], F32)
-        pose_sb = [sb(f"pose{a}", [P, 2, V], F32) for a in range(2)]
+        pose_sb = [sb("pose01", [P, 2, V], F32)]
+        pose_late = {t: sb(f"pose{t}", [P, V], F32) for t in (2, 3)}
         lg_sb = [sb(f"lg{a}", [P, 2, 2, V], F32) for a in range(2)]
         warm = sb("warm", [P, 1], F32)
 
         def load_rows(dst, src, z):
             nc.sync.dma_start(out=dst[:], in_=src[z * K_PASS : (z + 1) * K_PASS, :].rearrange("(p j) c -> p j c", j=PACK))
 
-        def load_words(z):
+        def load_words(z, lo=0, hi=T):
             nc.sync.dma_start(
-                out=xw_all[z][:].bitcast(I32), in_=x_words[z].rearrange("p n r -> p (n r)").bitcast(I32)
+                out=xw_all[z][:, lo:hi].bitcast(I32),
+                in_=x_words[z].rearrange("p n r -> p (n r)").bitcast(I32)[:, lo:hi],
             )
+
+        def load_pose(t):
+            nc.sync.dma_start(out=pose_late[t][:], in_=pose.rearrange("(p t) v -> p t v", t=PACK)[:, t, :])
 
         def load_pair(dst, src, a):
             nc.sync.dma_start(out=dst, in_=src.rearrange("(p t) v -> p t v", t=PACK)[:, 2 * a : 2 * a + 2, :])
@@ -62,7 +67,8 @@ def tile_picked_agree_none_p_kernel(
         nc.gpsimd.memset(xs_all[:].bitcast(I32), 0)
         nc.vector.memset(warm[:], 0.0)
         nc.scalar.activation(out=warm[:], in_=warm[:], func=SIGMOID)
-        load_rows(raw[0, 0], w1, 0)
+        load_words(0, 0, T // 2)
+        nc.sync.dma_start(offs_sb[:], offs)
         def load_scales(h):
             for r in (2 * h, 2 * h + 1):
                 for z in range(PASSES):
@@ -72,8 +78,8 @@ def tile_picked_agree_none_p_kernel(
                     )
 
         load_scales(0)
-        nc.sync.dma_start(offs_sb[:], offs)
-        load_words(0)
+        load_rows(raw[0, 0], w1, 0)
+        load_words(0, T // 2, T)
         load_scales(1)
         load_words(1)
         for h in range(2):
@@ -85,8 +91,9 @@ def tile_picked_agree_none_p_kernel(
         load_pair(pose_sb[0][:], pose, 0)
         nc.sync.dma_start(lists[1][:], p2)
         load_rows(raw[1, 0], w2, 0)
-        load_pair(pose_sb[1][:], pose, 1)
+        load_pose(2)
         load_rows(raw[1, 1], w2, 1)
+        load_pose(3)
         for a in range(2):
             load_pair(lg_sb[a][:, 0], lg1, a)
             load_pair(lg_sb[a][:, 1], lg2, a)
@@ -136,7 +143,7 @@ def tile_picked_agree_none_p_kernel(
         banks = {}
 
         bank_of = {(0, 0, 0): 0, (0, 0, S // 2): 1, (0, 1, 0): 2, (0, 2, 0): 3, (0, 3, 0): 4,
-                   (1, 0, 0): 5, (1, 1, 0): 6, (1, 2, 0): 7, (1, 3, 0): 0}
+                   (1, 0, 0): 5, (1, 1, 0): 6, (1, 2, 0): 5, (1, 3, 0): 6}
 
         def first_mm(w, z, t, lo=0, hi=S):
             if z == 0:
@@ -165,20 +172,17 @@ def tile_picked_agree_none_p_kernel(
 
         def gather_keys(t):
             for l in range(2):
-                if (t, l) == (3, 1):
-                    agree[t, l] = sb("agree_last", [P, V], F32, "grp110")[:]
                 nc.vector.tensor_tensor(
-                    agree[t, l], rows[0, t][:].indirect(lists[l][:]), pose_sb[t // 2][:, t % 2, :], MULT
+                    agree[t, l], rows[0, t][:].indirect(lists[l][:]), pose_late[t][:] if t > 1 else pose_sb[0][:, t, :], MULT
                 )
 
         def add_logits(a):
             if a == 0:
-                nc.vector.tensor_tensor(agree01[:], agree01[:], lg_sb[0][:], ADD)
+                for t in range(2):
+                    part = agree01[:, :, t, :]
+                    nc.vector.tensor_tensor(part, part, lg_sb[0][:, :, t, :], ADD)
             else:
-                flat = "p l t v -> p (l t v)"
-                first = agree23[:].rearrange(flat)[:, : 3 * V]
-                nc.vector.tensor_tensor(first, first, lg_sb[1][:].rearrange(flat)[:, : 3 * V], ADD)
-                nc.vector.tensor_tensor(agree23[:, 1, 1, :], agree[3, 1], lg_sb[1][:, 1, 1, :], ADD)
+                nc.vector.tensor_tensor(agree23[:], agree23[:], lg_sb[1][:], ADD)
 
         def sigmoid(t):
             nc.scalar.activation(out=gate[t][:], in_=(agree01, agree23)[t // 2][:, :, t % 2, :], func=SIGMOID)
@@ -270,26 +274,26 @@ def tile_picked_agree_none_p_kernel(
         gather_keys(1)
         evac(0, 3)
         cast(1, 0, 1, "scalar")
+        gather_keys(2)
         quant((1, 0, 0), 2 * P)
         first_mm(1, 0, 0)
         first_mm(1, 0, 1)
-        gather_keys(2)
-        cast(1, 1, 0, "scalar")
         quant((1, 0, 1), 2 * P)
-        first_mm(1, 0, 2)
-        first_mm(1, 0, 3)
+        cast(1, 1, 0, "scalar")
         quant((1, 1, 0), 2 * P)
         first_mm(1, 1, 0)
         first_mm(1, 1, 1)
         cast(1, 1, 1, "scalar")
         evac(1, 0)
         gather_keys(3)
-        quant((1, 1, 1), 2 * P)
-        first_mm(1, 1, 2)
-        first_mm(1, 1, 3)
         add_logits(0)
         sigmoid(0)
+        quant((1, 1, 1), 2 * P)
+        first_mm(1, 0, 2)
+        first_mm(1, 1, 2)
         evac(1, 1)
+        first_mm(1, 0, 3)
+        first_mm(1, 1, 3)
         sigmoid(1)
         add_logits(1)
         evac(1, 2)

@@ -64,7 +64,7 @@ def tile_picked_agree_none_p_kernel(
         def load_pair(dst, src, a):
             nc.sync.dma_start(out=dst, in_=src.rearrange("(p t) v -> p t v", t=PACK)[:, 2 * a : 2 * a + 2, :])
 
-        nc.gpsimd.memset(xs_all[:].bitcast(I32), 0)
+        nc.vector.memset(xs_all[:].bitcast(I32), 0)
         nc.vector.memset(warm[:], 0.0)
         nc.scalar.activation(out=warm[:], in_=warm[:], func=SIGMOID)
         load_words(0, 0, T // 2)

@@ -224,24 +224,25 @@ def tile_picked_agree_none_p_kernel(
             src = raw3[:, :, lo:hi].rearrange("p j (c i) -> p c j i", i=2)
             nc.scalar.copy(out=g[:, 0].rearrange("p (c i) j -> p c j i", i=2), in_=src)
 
-        def last_layer(lo, hi):
-            quant(("w3", lo), hi - lo)
-            for m0 in range(lo, hi, P):
-                block = m0 // P
-                cols = slice(m0 - lo, m0 - lo + P)
-                acc = psum.tile([P, V], F32, name=f"out{block}", tag=f"bank{1 + block}")
+        def last_layer(bank, blocks, first, end, engine):
+            n = len(blocks)
+            acc = psum.tile([P, n, end - first], F32, name=f"out{bank}", tag=f"bank{bank}")
+            for i, block in enumerate(blocks):
+                lo = max(start for start, stop in W3_PIECES if start <= block * P)
+                cols = slice(block * P - lo, (block + 1) * P - lo)
                 nc.tensor.matmul_mx(
-                    out=acc[:],
+                    out=acc[:, i, :],
                     lhsT=codes["w3", lo][:, cols].bitcast(FP8X4),
                     lhsT_scale=scales["w3", lo][:, cols],
-                    rhs=z_codes[:].bitcast(FP8X4),
-                    rhs_scale=z_scales[:],
+                    rhs=z_codes[:, first:end].bitcast(FP8X4),
+                    rhs_scale=z_scales[:, first:end],
                     start=True,
                     stop=True,
                 )
-                res = sb(f"res{block}", [P, V], F32)
-                copy_on("vector" if block % 2 else "scalar", res[:], acc[:])
-                nc.sync.dma_start(out=out[m0 : m0 + P, :], in_=res[:])
+            res = sb(f"res{bank}", [P, n, end - first], F32)
+            copy_on(engine, res[:], acc[:])
+            rows_out = out[blocks[0] * P : (blocks[0] + n) * P, first:end]
+            nc.sync.dma_start(out=rows_out.rearrange("(b p) v -> p b v", p=P), in_=res[:])
 
         cast(0, 0, 0, "scalar")
         cast(0, 0, 1, "scalar")
@@ -311,4 +312,8 @@ def tile_picked_agree_none_p_kernel(
         for h in range(2):
             quant_z(h)
         for lo, hi in W3_PIECES:
-            last_layer(lo, hi)
+            quant(("w3", lo), hi - lo)
+        last_layer(1, (0, 1), 0, HALF, "scalar")
+        last_layer(2, (0, 1), HALF, V, "vector")
+        last_layer(3, (2,), 0, V, "scalar")
+        last_layer(4, (3,), 0, V, "vector")

@@ -1,6 +1,7 @@
 from contextlib import ExitStack
 
 import concourse.mybir as mybir
+from concourse.masks import make_identity
 
 K, T, S, V, N, H = 1024, 2048, 512, 256, 512, 512
 FLOPS = 2 * (2 * K * H * S + H * N * V)
@@ -15,6 +16,7 @@ FP8X4 = mybir.dt.float8_e4m3fn_x4
 MULT = mybir.AluOpType.mult
 ADD = mybir.AluOpType.add
 SIGMOID = mybir.ActivationFunctionType.Sigmoid
+COPY = mybir.ActivationFunctionType.Copy
 
 P = 128
 PACK = 4
@@ -44,10 +46,11 @@ def tile_picked_agree_none_p_kernel(
         raw = {(w, z): sb(f"raw{w}{z}", [P, PACK, H], F32) for w in range(2) for z in range(PASSES) if (w, z) != (0, 1)}
         late = [sb(f"late{h}", [P, 2, H], F32) for h in range(2)]
         raw3 = sb("raw3", [P, PACK, N], F32)
-        pose_sb = [sb("pose01", [P, 2, V], F32)]
-        pose_late = {t: sb(f"pose{t}", [P, V], F32) for t in (2, 3)}
+        pose_sb = [sb(f"pose{a}", [P, 2, V], F32) for a in range(2)]
         lg_sb = [sb(f"lg{a}", [P, 2, 2, V], F32) for a in range(2)]
         warm = sb("warm", [P, 1], F32)
+        ident = sb("ident", [P, P], F32)
+        make_identity(nc, ident[:])
 
         def load_rows(dst, src, z):
             nc.sync.dma_start(out=dst[:], in_=src[z * K_PASS : (z + 1) * K_PASS, :].rearrange("(p j) c -> p j c", j=PACK))
@@ -57,9 +60,6 @@ def tile_picked_agree_none_p_kernel(
                 out=xw_all[z][:, lo:hi].bitcast(I32),
                 in_=x_words[z].rearrange("p n r -> p (n r)").bitcast(I32)[:, lo:hi],
             )
-
-        def load_pose(t):
-            nc.sync.dma_start(out=pose_late[t][:], in_=pose.rearrange("(p t) v -> p t v", t=PACK)[:, t, :])
 
         def load_pair(dst, src, a):
             nc.sync.dma_start(out=dst, in_=src.rearrange("(p t) v -> p t v", t=PACK)[:, 2 * a : 2 * a + 2, :])
@@ -82,18 +82,17 @@ def tile_picked_agree_none_p_kernel(
         load_words(0, T // 2, T)
         load_scales(1)
         load_words(1)
+        nc.sync.dma_start(lists[0][:], p1)
+        nc.sync.dma_start(lists[1][:], p2)
         for h in range(2):
             nc.sync.dma_start(
                 out=late[h][:],
                 in_=w1[K_PASS:, :].rearrange("(p j) c -> p j c", j=PACK)[:, 2 * h : 2 * h + 2, :],
             )
-        nc.sync.dma_start(lists[0][:], p1)
         load_pair(pose_sb[0][:], pose, 0)
-        nc.sync.dma_start(lists[1][:], p2)
         load_rows(raw[1, 0], w2, 0)
-        load_pose(2)
         load_rows(raw[1, 1], w2, 1)
-        load_pose(3)
+        load_pair(pose_sb[1][:], pose, 1)
         for a in range(2):
             load_pair(lg_sb[a][:, 0], lg1, a)
             load_pair(lg_sb[a][:, 1], lg2, a)
@@ -121,6 +120,24 @@ def tile_picked_agree_none_p_kernel(
             flat = g[:].rearrange("p b m j -> p (b m j)")
             nc.vector.quantize_mx(out=codes[key][:].bitcast(FP8X4), scales=scales[key][:], in_=flat)
 
+        both = sb("both", [P, PASSES, 2, P, PACK], BF16)
+        both_codes = sb("both_codes", [P, PASSES, 2 * P], U32)
+        both_scales = sb("both_scales", [P, PASSES, 2 * P], U8)
+
+        def cast_both(z, engine):
+            src = raw[1, z][:].rearrange("p j (m a b) -> p a m j b", a=2, b=2)[:, 1]
+            copy_on(engine, both[:, z].rearrange("p b m j -> p m j b"), src)
+
+        def quant_both():
+            nc.vector.quantize_mx(
+                out=both_codes[:].rearrange("p z c -> p (z c)").bitcast(FP8X4),
+                scales=both_scales[:].rearrange("p z c -> p (z c)"),
+                in_=both[:].rearrange("p z b m j -> p (z b m j)"),
+            )
+            for z in range(PASSES):
+                codes[1, z, 1] = both_codes[:, z]
+                scales[1, z, 1] = both_scales[:, z]
+
         for a in range(2):
             grouped[0, 1, a] = sb(f"grp01{a}", [P, 2, P, PACK], BF16)
             codes[0, 1, a] = sb(f"codes01{a}", [P, 2 * P], U32)
@@ -131,8 +148,8 @@ def tile_picked_agree_none_p_kernel(
             dst = grouped[0, 1, a][:, :, lo:hi, 2 * h : 2 * h + 2]
             copy_on(engine, dst.rearrange("p b m j -> p m j b"), src)
 
-        def late_quant(t):
-            key, b = (0, 1, t // 2), t % 2
+        def late_quant(t, w=0):
+            key, b = (w, 1, t // 2), t % 2
             cols = slice(b * P, (b + 1) * P)
             nc.vector.quantize_mx(
                 out=codes[key][:, cols].bitcast(FP8X4),
@@ -143,7 +160,7 @@ def tile_picked_agree_none_p_kernel(
         banks = {}
 
         bank_of = {(0, 0, 0): 0, (0, 0, S // 2): 1, (0, 1, 0): 2, (0, 2, 0): 3, (0, 3, 0): 4,
-                   (1, 0, 0): 5, (1, 1, 0): 6, (1, 2, 0): 5, (1, 3, 0): 6}
+                   (1, 0, 0): 5, (1, 0, S // 2): 6, (1, 1, 0): 7, (1, 2, 0): 0, (1, 3, 0): 1}
 
         def first_mm(w, z, t, lo=0, hi=S):
             if z == 0:
@@ -159,33 +176,64 @@ def tile_picked_agree_none_p_kernel(
                 stop=(z == PASSES - 1),
             )
 
-        rows = {(w, t): sb(f"rows{w}{t}", [P, S], F32) for w in range(2) for t in range(PACK)}
+        rows = {}
 
-        def evac(w, t, lo=0, hi=S):
-            nc.scalar.copy(out=rows[w, t][:, lo:hi], in_=banks[w, t, lo][:])
+        def evac(w, t, lo=0, hi=S, tag=None, engine="scalar"):
+            if lo == 0:
+                rows[w, t] = sb(f"rows{w}{t}", [P, S], F32, tag)
+            copy_on(engine, rows[w, t][:, lo:hi], banks[w, t, lo][:])
 
-        agree01 = sb("agree01", [P, 2, 2, V], F32)
-        agree23 = sb("agree23", [P, 2, 2, V], F32)
-        agree = {(t, l): (agree01, agree23)[t // 2][:, l, t % 2, :] for t in range(PACK) for l in range(2)}
+        agree_pair = [sb(f"agree{t}", [P, 2, V], F32) for t in range(PACK - 1)]
+        agree = {(t, l): agree_pair[t][:, l, :] for t in range(PACK - 1) for l in range(2)}
         gate = [sb(f"gate{t}", [P, 2, V], F32) for t in range(PACK)]
         votes = sb("votes", [P, 2, PACK, V], F32)
 
+        def gather_key(t, l, tag=None):
+            if t == PACK - 1:
+                agree[t, l] = sb(f"agree{t}{l}", [P, V], F32, tag)[:]
+            nc.vector.tensor_tensor(agree[t, l], rows[0, t][:].indirect(lists[l][:]), pose_sb[t // 2][:, t % 2, :], MULT)
+
         def gather_keys(t):
             for l in range(2):
-                nc.vector.tensor_tensor(
-                    agree[t, l], rows[0, t][:].indirect(lists[l][:]), pose_late[t][:] if t > 1 else pose_sb[0][:, t, :], MULT
-                )
+                gather_key(t, l)
 
-        def add_logits(a):
-            if a == 0:
-                for t in range(2):
-                    part = agree01[:, :, t, :]
-                    nc.vector.tensor_tensor(part, part, lg_sb[0][:, :, t, :], ADD)
-            else:
-                nc.vector.tensor_tensor(agree23[:], agree23[:], lg_sb[1][:], ADD)
+        def add_logits(t):
+            part = agree_pair[t][:]
+            nc.vector.tensor_tensor(part, part, lg_sb[t // 2][:, :, t % 2, :], ADD)
 
         def sigmoid(t):
-            nc.scalar.activation(out=gate[t][:], in_=(agree01, agree23)[t // 2][:, :, t % 2, :], func=SIGMOID)
+            nc.scalar.activation(out=gate[t][:], in_=agree_pair[t][:], func=SIGMOID)
+
+        logit, gate_bank, fetched = {}, {}, {}
+
+        def turn(dst, src, start, stop):
+            nc.tensor.matmul(dst, lhsT=src, rhs=ident[:], start=start, stop=stop, is_transpose=True)
+
+        def turned_logits(t, bank):
+            logit[t] = psum.tile([P, 2, V], F32, name=f"logit{t}", tag=f"bank{bank}")
+            for l in range(2):
+                for h in range(2):
+                    cols = slice(h * HALF, (h + 1) * HALF)
+                    turn(logit[t][:, l, cols], lg_sb[t // 2][:, l, t % 2, cols], True, False)
+                    turn(logit[t][:, l, cols], agree[t, l][:, cols], False, True)
+
+        def turned_sigmoid(t):
+            nc.scalar.activation(out=gate[t][:], in_=logit[t][:], func=SIGMOID)
+
+        def turn_back(t):
+            gate_bank[t] = psum.tile([P, 2, V], F32, name=f"gateb{t}", tag=f"bank{4 + t // 2}")
+            for l in range(2):
+                for h in range(2):
+                    cols = slice(h * HALF, (h + 1) * HALF)
+                    turn(gate_bank[t][:, l, cols], gate[t][:, l, cols], True, True)
+
+        def fetch_votes(t, tag=None):
+            fetched[t] = sb(f"fetched{t}", [P, 2, V], F32, tag)
+            for l in range(2):
+                nc.scalar.activation(out=fetched[t][:, l, :], in_=rows[1, t][:].indirect(lists[l][:]), func=COPY)
+
+        def weigh(t, lo, hi):
+            nc.vector.tensor_tensor(votes[:, :, t, lo:hi], fetched[t][:, :, lo:hi], gate_bank[t][:, :, lo:hi], MULT)
 
         def gather_votes(t, lo, hi):
             for l in range(2):
@@ -204,9 +252,9 @@ def tile_picked_agree_none_p_kernel(
             cols = slice(h * HALF, (h + 1) * HALF)
             walk = "p t (c i) -> p c t i"
             nc.vector.tensor_tensor(
-                z_grouped[:, cols, :].rearrange("p (c i) t -> p c t i", i=2),
-                votes[:, 0, :, cols].rearrange(walk, i=2),
-                votes[:, 1, :, cols].rearrange(walk, i=2),
+                z_grouped[:, cols, :].rearrange("p (c i) t -> p c t i", i=4),
+                votes[:, 0, :, cols].rearrange(walk, i=4),
+                votes[:, 1, :, cols].rearrange(walk, i=4),
                 ADD,
             )
 
@@ -218,11 +266,13 @@ def tile_picked_agree_none_p_kernel(
                 in_=z_grouped[:, cols, :].rearrange("p v t -> p (v t)"),
             )
 
-        def cast3(lo, hi):
-            g = sb(f"grp3{lo}", [P, 1, hi - lo, PACK], BF16)
+        def cast3(lo, hi, engine):
+            if lo == 0:
+                grouped["w3"] = sb("grp3", [P, 1, N, PACK], BF16, "lg1")
+            g = grouped["w3"][:, :, lo:hi]
             grouped["w3", lo] = g
-            src = raw3[:, :, lo:hi].rearrange("p j (c i) -> p c j i", i=2)
-            nc.scalar.copy(out=g[:, 0].rearrange("p (c i) j -> p c j i", i=2), in_=src)
+            src = raw3[:, :, lo:hi].rearrange("p j (c i) -> p c j i", i=4)
+            copy_on(engine, g[:, 0].rearrange("p (c i) j -> p c j i", i=4), src)
 
         def last_layer(bank, blocks, first, end, engine):
             n = len(blocks)
@@ -270,50 +320,60 @@ def tile_picked_agree_none_p_kernel(
             first_mm(0, 1, t)
         evac(0, 1)
         gather_keys(0)
-        evac(0, 2)
         cast(1, 0, 0, "scalar")
         gather_keys(1)
-        evac(0, 3)
-        cast(1, 0, 1, "scalar")
-        gather_keys(2)
+        cast_both(0, "scalar")
+        evac(0, 2)
         quant((1, 0, 0), 2 * P)
-        first_mm(1, 0, 0)
-        first_mm(1, 0, 1)
-        quant((1, 0, 1), 2 * P)
-        cast(1, 1, 0, "scalar")
-        quant((1, 1, 0), 2 * P)
-        first_mm(1, 1, 0)
-        first_mm(1, 1, 1)
-        cast(1, 1, 1, "scalar")
-        evac(1, 0)
-        gather_keys(3)
+        cast(1, 1, 0, "vector")
+        cast_both(1, "scalar")
+        evac(0, 3)
+        codes[1, 1, 0] = sb("codes110", [P, 2 * P], U32)
+        scales[1, 1, 0] = sb("scales110", [P, 2 * P], U8)
+        late_quant(0, 1)
+        late_quant(1, 1)
+        for z in range(PASSES):
+            first_mm(1, z, 0, 0, S // 2)
+            first_mm(1, z, 0, S // 2, S)
+            first_mm(1, z, 1)
+        gather_key(2, 0)
+        quant_both()
         add_logits(0)
-        sigmoid(0)
-        quant((1, 1, 1), 2 * P)
-        first_mm(1, 0, 2)
-        first_mm(1, 1, 2)
+        gather_key(2, 1)
+        gather_keys(3)
+        add_logits(2)
+        turned_logits(1, 2)
+        for t in (2, 3):
+            first_mm(1, 0, t)
+            first_mm(1, 1, t)
+        evac(1, 0, 0, S // 2)
+        evac(1, 0, S // 2, S)
         evac(1, 1)
-        first_mm(1, 0, 3)
-        first_mm(1, 1, 3)
-        sigmoid(1)
-        add_logits(1)
+        sigmoid(0)
+        fetch_votes(1)
+        turned_sigmoid(1)
+        turned_logits(3, 3)
+        turn_back(1)
         evac(1, 2)
         sigmoid(2)
-        evac(1, 3)
-        sigmoid(3)
+        gather_votes(0, 0, V)
+        evac(1, 3, engine="vector")
+        turned_sigmoid(3)
+        turn_back(3)
+        fetch_votes(3, "agree31")
         for lo, hi in W3_PIECES:
-            cast3(lo, hi)
-        for t in range(PACK - 1):
-            gather_votes(t, 0, V)
+            cast3(lo, hi, "scalar")
+        weigh(1, 0, V)
+        gather_votes(2, 0, V)
         for h in range(2):
-            gather_votes(PACK - 1, h * HALF, (h + 1) * HALF)
+            weigh(3, h * HALF, (h + 1) * HALF)
         for h in range(2):
             sum_votes(h)
         for h in range(2):
             quant_z(h)
         for lo, hi in W3_PIECES:
             quant(("w3", lo), hi - lo)
-        last_layer(1, (0, 1), 0, HALF, "scalar")
-        last_layer(2, (0, 1), HALF, V, "vector")
-        last_layer(3, (2,), 0, V, "scalar")
-        last_layer(4, (3,), 0, V, "vector")
+        last_layer(6, (0, 1), 0, HALF, "scalar")
+        last_layer(7, (0, 1), HALF, V, "vector")
+        last_layer(0, (2,), 0, V, "scalar")
+        last_layer(1, (3,), 0, V, "vector")

@@ -61,6 +61,12 @@ def tile_picked_agree_none_p_kernel(
                 in_=x_words[z].rearrange("p n r -> p (n r)").bitcast(I32)[:, lo:hi],
             )
 
+        def load_row_pair(h):
+            nc.sync.dma_start(
+                out=late[h][:],
+                in_=w1[K_PASS:, :].rearrange("(p j) c -> p j c", j=PACK)[:, 2 * h : 2 * h + 2, :],
+            )
+
         def load_pair(dst, src, a):
             nc.sync.dma_start(out=dst, in_=src.rearrange("(p t) v -> p t v", t=PACK)[:, 2 * a : 2 * a + 2, :])
 
@@ -82,13 +88,10 @@ def tile_picked_agree_none_p_kernel(
         load_words(0, T // 2, T)
         load_scales(1)
         load_words(1)
+        load_row_pair(0)
         nc.sync.dma_start(lists[0][:], p1)
         nc.sync.dma_start(lists[1][:], p2)
-        for h in range(2):
-            nc.sync.dma_start(
-                out=late[h][:],
-                in_=w1[K_PASS:, :].rearrange("(p j) c -> p j c", j=PACK)[:, 2 * h : 2 * h + 2, :],
-            )
+        load_row_pair(1)
         load_pair(pose_sb[0][:], pose, 0)
         load_rows(raw[1, 0], w2, 0)
         load_rows(raw[1, 1], w2, 1)

@@ -23,7 +23,6 @@ PACK = 4
 K_PASS = P * PACK
 PASSES = K // K_PASS
 HALF = V // 2
-W3_PIECES = ((0, 256), (256, 384), (384, 512))
 
 
 def tile_picked_agree_none_p_kernel(
@@ -32,10 +31,16 @@ def tile_picked_agree_none_p_kernel(
     nc = tc.nc
     with ExitStack() as ctx:
         keep = ctx.enter_context(tc.tile_pool(name="keep", bufs=1))
+        shared = ctx.enter_context(tc.tile_pool(name="shared", bufs=1))
         psum = ctx.enter_context(tc.psum_pool(name="psum", bufs=1))
 
         def sb(name, shape, dtype, tag=None):
+            if isinstance(tag, int):
+                return shared.tile(shape, dtype, name=name, tag=name, align_bytes=64, offset=tag)
             return keep.tile(shape, dtype, name=name, tag=tag or name, align_bytes=64)
+
+        def bank(name, shape, b):
+            return psum.tile(shape, F32, name=name, tag=f"bank{b}")
 
         offs_sb = sb("offs_sb", [P, S // 16], U16)
         lists = [sb("p1_sb", [P, V // 16], U16), sb("p2_sb", [P, V // 16], U16)]
@@ -43,10 +48,10 @@ def tile_picked_agree_none_p_kernel(
         xw_all = [sb(f"xw_all{z}", [P, T], U32) for z in range(PASSES)]
         xs = sb("xs", [P, S], U8)
         xw = [sb(f"xw{z}", [P, S], U32) for z in range(PASSES)]
-        raw = {(w, z): sb(f"raw{w}{z}", [P, PACK, H], F32) for w in range(2) for z in range(PASSES) if (w, z) != (0, 1)}
-        late = [sb(f"late{h}", [P, 2, H], F32) for h in range(2)]
+        raw = {(w, z): sb(f"raw{w}{z}", [P, PACK, H], F32) for w in range(2) for z in range(PASSES)}
         raw3 = sb("raw3", [P, PACK, N], F32)
-        pose_sb = [sb(f"pose{a}", [P, 2, V], F32) for a in range(2)]
+        pose_parts = {lo: sb(f"pose{lo}", [P, hi - lo, V], F32) for lo, hi in ((0, 1), (1, 3), (3, 4))}
+        pose_of = [pose_parts[0][:, 0:1], pose_parts[1][:, 0:1], pose_parts[1][:, 1:2], pose_parts[3][:, 0:1]]
         lg_sb = [sb(f"lg{a}", [P, 2, 2, V], F32) for a in range(2)]
         warm = sb("warm", [P, 1], F32)
         ident = sb("ident", [P, P], F32)
@@ -61,20 +66,12 @@ def tile_picked_agree_none_p_kernel(
                 in_=x_words[z].rearrange("p n r -> p (n r)").bitcast(I32)[:, lo:hi],
             )
 
-        def load_row_pair(h):
-            nc.sync.dma_start(
-                out=late[h][:],
-                in_=w1[K_PASS:, :].rearrange("(p j) c -> p j c", j=PACK)[:, 2 * h : 2 * h + 2, :],
-            )
-
         def load_pair(dst, src, a):
             nc.sync.dma_start(out=dst, in_=src.rearrange("(p t) v -> p t v", t=PACK)[:, 2 * a : 2 * a + 2, :])
 
-        nc.vector.memset(xs_all[:].bitcast(I32), 0)
-        nc.vector.memset(warm[:], 0.0)
-        nc.scalar.activation(out=warm[:], in_=warm[:], func=SIGMOID)
-        load_words(0, 0, T // 2)
-        nc.sync.dma_start(offs_sb[:], offs)
+        def load_poses(lo, hi):
+            nc.sync.dma_start(out=pose_parts[lo][:], in_=pose.rearrange("(p t) v -> p t v", t=PACK)[:, lo:hi, :])
+
         def load_scales(h):
             for r in (2 * h, 2 * h + 1):
                 for z in range(PASSES):
@@ -83,25 +80,51 @@ def tile_picked_agree_none_p_kernel(
                         in_=x_scales[z, r : 16 : 4, :].bitcast(I32),
                     )
 
-        load_scales(0)
-        load_rows(raw[0, 0], w1, 0)
-        load_words(0, T // 2, T)
-        load_scales(1)
-        load_words(1)
-        load_row_pair(0)
-        nc.sync.dma_start(lists[0][:], p1)
-        nc.sync.dma_start(lists[1][:], p2)
-        load_row_pair(1)
-        load_pair(pose_sb[0][:], pose, 0)
-        load_rows(raw[1, 0], w2, 0)
-        load_rows(raw[1, 1], w2, 1)
-        load_pair(pose_sb[1][:], pose, 1)
-        for a in range(2):
+        def load_logits(a):
             load_pair(lg_sb[a][:, 0], lg1, a)
             load_pair(lg_sb[a][:, 1], lg2, a)
-        load_rows(raw3, w3, 0)
 
-        grouped, codes, scales = {}, {}, {}
+        nc.vector.memset(xs_all[:].bitcast(I32), 0)
+        nc.vector.memset(warm[:], 0.0)
+        nc.scalar.activation(out=warm[:], in_=warm[:], func=SIGMOID)
+        load_words(0, 0, T // 2)
+        nc.sync.dma_start(offs_sb[:], offs)
+        load_scales(0)
+        load_words(0, T // 2, T)
+        load_rows(raw[0, 0], w1, 0)
+        load_scales(1)
+        load_rows(raw[0, 1], w1, 1)
+        load_words(1)
+        load_rows(raw[1, 0], w2, 0)
+        nc.sync.dma_start(lists[0][:], p1)
+        load_poses(0, 1)
+        nc.sync.dma_start(lists[1][:], p2)
+        load_rows(raw[1, 1], w2, 1)
+        load_poses(1, 3)
+        load_poses(3, 4)
+        load_pair(lg_sb[0][:, 0], lg1, 0)
+        load_pair(lg_sb[0][:, 1], lg2, 0)
+        load_rows(raw3, w3, 0)
+        load_logits(1)
+
+        keys = [(w, z) for w in range(2) for z in range(PASSES)]
+        grouped = {(w, z, 0): sb(f"grp{w}{z}", [P, 2, P, PACK], BF16)[:] for w, z in keys}
+        codes = {(w, z, 0): sb(f"codes{w}{z}", [P, 2 * P], U32)[:] for w, z in keys[1:]}
+        scales = {(w, z, 0): sb(f"scales{w}{z}", [P, 2 * P], U8)[:] for w, z in keys}
+        late = [sb(f"late{w}", [P, PASSES, 2, P, PACK], BF16) for w in range(2)]
+        late_codes = [sb(f"late_codes{w}", [P, PASSES, 2 * P], U32) for w in range(2)]
+        late_scales = [sb(f"late_scales{w}", [P, PASSES, 2 * P], U8) for w in range(2)]
+        for w, z in keys:
+            grouped[w, z, 1] = late[w][:, z]
+            codes[w, z, 1] = late_codes[w][:, z]
+            scales[w, z, 1] = late_scales[w][:, z]
+
+        def quant_late(w):
+            nc.vector.quantize_mx(
+                out=late_codes[w][:].rearrange("p z c -> p (z c)").bitcast(FP8X4),
+                scales=late_scales[w][:].rearrange("p z c -> p (z c)"),
+                in_=late[w][:].rearrange("p z b m j -> p (z b m j)"),
+            )
 
         def copy_on(engine, out_ap, in_ap):
             if engine == "vector":
@@ -109,65 +132,28 @@ def tile_picked_agree_none_p_kernel(
             else:
                 nc.scalar.copy(out=out_ap, in_=in_ap)
 
-        def cast(w, z, a, engine):
-            g = sb(f"grp{w}{z}{a}", [P, 2, P, PACK], BF16)
-            grouped[w, z, a] = g
-            src = raw[w, z][:].rearrange("p j (m a b) -> p a m j b", a=2, b=2)[:, a]
-            copy_on(engine, g[:].rearrange("p b m j -> p m j b"), src)
+        def cast(w, z, a, engine, lo=0, hi=P):
+            src = raw[w, z][:].rearrange("p j (m a b) -> p a m j b", a=2, b=2)[:, a, lo:hi]
+            copy_on(engine, grouped[w, z, a][:, :, lo:hi].rearrange("p b m j -> p m j b"), src)
 
-        def quant(key, width):
-            name = "".join(str(x) for x in key)
-            codes[key] = sb(f"codes{name}", [P, width], U32)
-            scales[key] = sb(f"scales{name}", [P, width], U8)
-            g = grouped[key]
-            flat = g[:].rearrange("p b m j -> p (b m j)")
-            nc.vector.quantize_mx(out=codes[key][:].bitcast(FP8X4), scales=scales[key][:], in_=flat)
-
-        both = sb("both", [P, PASSES, 2, P, PACK], BF16)
-        both_codes = sb("both_codes", [P, PASSES, 2 * P], U32)
-        both_scales = sb("both_scales", [P, PASSES, 2 * P], U8)
-
-        def cast_both(z, engine):
-            src = raw[1, z][:].rearrange("p j (m a b) -> p a m j b", a=2, b=2)[:, 1]
-            copy_on(engine, both[:, z].rearrange("p b m j -> p m j b"), src)
-
-        def quant_both():
+        def quant(w, z, a, b0=0, b1=2):
+            cols = slice(b0 * P, b1 * P)
             nc.vector.quantize_mx(
-                out=both_codes[:].rearrange("p z c -> p (z c)").bitcast(FP8X4),
-                scales=both_scales[:].rearrange("p z c -> p (z c)"),
-                in_=both[:].rearrange("p z b m j -> p (z b m j)"),
+                out=codes[w, z, a][:, cols].bitcast(FP8X4),
+                scales=scales[w, z, a][:, cols],
+                in_=grouped[w, z, a][:, b0:b1].rearrange("p b m j -> p (b m j)"),
             )
-            for z in range(PASSES):
-                codes[1, z, 1] = both_codes[:, z]
-                scales[1, z, 1] = both_scales[:, z]
 
-        for a in range(2):
-            grouped[0, 1, a] = sb(f"grp01{a}", [P, 2, P, PACK], BF16)
-            codes[0, 1, a] = sb(f"codes01{a}", [P, 2 * P], U32)
-            scales[0, 1, a] = sb(f"scales01{a}", [P, 2 * P], U8)
-
-        def late_cast(h, a, engine, lo, hi):
-            src = late[h][:].rearrange("p j (m a b) -> p a m j b", a=2, b=2)[:, a, lo:hi]
-            dst = grouped[0, 1, a][:, :, lo:hi, 2 * h : 2 * h + 2]
-            copy_on(engine, dst.rearrange("p b m j -> p m j b"), src)
-
-        def late_quant(t, w=0):
-            key, b = (w, 1, t // 2), t % 2
-            cols = slice(b * P, (b + 1) * P)
-            nc.vector.quantize_mx(
-                out=codes[key][:, cols].bitcast(FP8X4),
-                scales=scales[key][:, cols],
-                in_=grouped[key][:, b].rearrange("p m j -> p (m j)"),
-            )
+        def gather_words(z, lo, hi):
+            nc.vector.tensor_copy(xw[z][:, lo:hi], xw_all[z][:].indirect(offs_sb[:, lo // 16 : hi // 16]))
 
         banks = {}
-
-        bank_of = {(0, 0, 0): 0, (0, 0, S // 2): 1, (0, 1, 0): 2, (0, 2, 0): 3, (0, 3, 0): 4,
-                   (1, 0, 0): 5, (1, 0, S // 2): 6, (1, 1, 0): 7, (1, 2, 0): 0, (1, 3, 0): 1}
+        bank_of = {(0, t, h * S // 2): PACK * h + t for t in range(PACK) for h in range(2)}
+        bank_of.update({(1, 0, 0): 0, (1, 0, S // 2): 1, (1, 1, 0): 2, (1, 2, 0): 3, (1, 3, 0): 4})
 
         def first_mm(w, z, t, lo=0, hi=S):
             if z == 0:
-                banks[w, t, lo] = psum.tile([P, hi - lo], F32, name=f"acc{w}{t}{lo}", tag=f"bank{bank_of[w, t, lo]}")
+                banks[w, t, lo] = bank(f"acc{w}{t}{lo}", [P, hi - lo], bank_of[w, t, lo])
             key, cols = (w, z, t // 2), slice(P * (t % 2), P * (t % 2 + 1))
             nc.tensor.matmul_mx(
                 out=banks[w, t, lo][:],
@@ -179,73 +165,85 @@ def tile_picked_agree_none_p_kernel(
                 stop=(z == PASSES - 1),
             )
 
-        rows = {}
+        rows = {(w, t): sb(f"rows{w}{t}", [P, S], F32) for w in range(2) for t in range(PACK)}
 
-        def evac(w, t, lo=0, hi=S, tag=None, engine="scalar"):
-            if lo == 0:
-                rows[w, t] = sb(f"rows{w}{t}", [P, S], F32, tag)
+        def evac(w, t, engine, lo=0, hi=S):
             copy_on(engine, rows[w, t][:, lo:hi], banks[w, t, lo][:])
 
-        agree_pair = [sb(f"agree{t}", [P, 2, V], F32) for t in range(PACK - 1)]
-        agree = {(t, l): agree_pair[t][:, l, :] for t in range(PACK - 1) for l in range(2)}
+        agree = [sb(f"agree{t}", [P, 2, V], F32) for t in range(PACK - 1)] + [sb("agree3", [P, 2, V], F32, 0)]
         gate = [sb(f"gate{t}", [P, 2, V], F32) for t in range(PACK)]
-        votes = sb("votes", [P, 2, PACK, V], F32)
 
-        def gather_key(t, l, tag=None):
-            if t == PACK - 1:
-                agree[t, l] = sb(f"agree{t}{l}", [P, V], F32, tag)[:]
-            nc.vector.tensor_tensor(agree[t, l], rows[0, t][:].indirect(lists[l][:]), pose_sb[t // 2][:, t % 2, :], MULT)
+        plain_keys = {}
 
-        def gather_keys(t):
-            for l in range(2):
-                gather_key(t, l)
+        def gather_keys(t, children=(0, 1)):
+            for l in children:
+                nc.vector.tensor_tensor(
+                    agree[t][:, l, :], rows[0, t][:].indirect(lists[l][:]), pose_of[t][:, 0, :], MULT
+                )
 
-        def add_logits(t):
-            part = agree_pair[t][:]
-            nc.vector.tensor_tensor(part, part, lg_sb[t // 2][:, :, t % 2, :], ADD)
+        def fetch_key(t, l, tag):
+            plain_keys[t, l] = sb(f"plain_key{t}{l}", [P, V], F32, tag)
+            nc.scalar.activation(out=plain_keys[t, l][:], in_=rows[0, t][:].indirect(lists[l][:]), func=COPY)
 
-        def sigmoid(t):
-            nc.scalar.activation(out=gate[t][:], in_=agree_pair[t][:], func=SIGMOID)
+        def pose_key(t, l):
+            nc.vector.tensor_tensor(agree[t][:, l, :], plain_keys[t, l][:], pose_of[t][:, 0, :], MULT)
 
         logit, gate_bank, fetched = {}, {}, {}
+        logit_bank = (0, 1, 2, 5)
+        back_bank = (6, 7, 1, 0)
 
         def turn(dst, src, start, stop):
             nc.tensor.matmul(dst, lhsT=src, rhs=ident[:], start=start, stop=stop, is_transpose=True)
 
-        def turned_logits(t, bank):
-            logit[t] = psum.tile([P, 2, V], F32, name=f"logit{t}", tag=f"bank{bank}")
+        def turned_logits(t):
+            logit[t] = bank(f"logit{t}", [P, 2, V], logit_bank[t])
             for l in range(2):
                 for h in range(2):
                     cols = slice(h * HALF, (h + 1) * HALF)
                     turn(logit[t][:, l, cols], lg_sb[t // 2][:, l, t % 2, cols], True, False)
-                    turn(logit[t][:, l, cols], agree[t, l][:, cols], False, True)
+                    turn(logit[t][:, l, cols], agree[t][:, l, cols], False, True)
 
-        def turned_sigmoid(t):
+        def sigmoid(t):
             nc.scalar.activation(out=gate[t][:], in_=logit[t][:], func=SIGMOID)
 
         def turn_back(t):
-            gate_bank[t] = psum.tile([P, 2, V], F32, name=f"gateb{t}", tag=f"bank{4 + t // 2}")
-            for l in range(2):
-                for h in range(2):
+            gate_bank[t] = bank(f"gateb{t}", [P, 2, V], back_bank[t])
+            for h in range(2):
+                for l in range(2):
                     cols = slice(h * HALF, (h + 1) * HALF)
                     turn(gate_bank[t][:, l, cols], gate[t][:, l, cols], True, True)
 
-        def fetch_votes(t, tag=None):
-            fetched[t] = sb(f"fetched{t}", [P, 2, V], F32, tag)
-            for l in range(2):
-                nc.scalar.activation(out=fetched[t][:, l, :], in_=rows[1, t][:].indirect(lists[l][:]), func=COPY)
+        def fetch(t, lo=0, hi=V, tag=None, children=(0, 1)):
+            fetched[t, lo] = sb(f"fetched{t}{lo}", [P, 2, hi - lo], F32, tag)
+            for l in children:
+                nc.scalar.activation(
+                    out=fetched[t, lo][:, l, :],
+                    in_=rows[1, t][:].indirect(lists[l][:, lo // 16 : hi // 16]),
+                    func=COPY,
+                )
 
-        def weigh(t, lo, hi):
-            nc.vector.tensor_tensor(votes[:, :, t, lo:hi], fetched[t][:, :, lo:hi], gate_bank[t][:, :, lo:hi], MULT)
-
-        def gather_votes(t, lo, hi):
+        def fetch_on_vector(t):
+            fetched[t, 0] = sb(f"fetched{t}0", [P, 2, V], F32)
             for l in range(2):
+                nc.vector.tensor_copy(fetched[t, 0][:, l, :], rows[1, t][:].indirect(lists[l][:]))
+
+        def add_logits(t):
+            nc.vector.tensor_tensor(agree[t][:], agree[t][:], lg_sb[t // 2][:, :, t % 2, :], ADD)
+
+        def plain_sigmoid(t):
+            nc.scalar.activation(out=gate[t][:], in_=agree[t][:], func=SIGMOID)
+
+        def gather_votes(t, lo=0, hi=V, children=(0, 1)):
+            for l in children:
                 nc.vector.tensor_tensor(
                     votes[:, l, t, lo:hi],
                     rows[1, t][:].indirect(lists[l][:, lo // 16 : hi // 16]),
                     gate[t][:, l, lo:hi],
                     MULT,
                 )
+
+        def weigh(t, lo=0, hi=V):
+            nc.vector.tensor_tensor(votes[:, :, t, lo:hi], fetched[t, lo][:], gate_bank[t][:, :, lo:hi], MULT)
 
         z_grouped = sb("z_grouped", [P, V, PACK], BF16)
         z_codes = sb("z_codes", [P, V], U32)
@@ -269,114 +267,130 @@ def tile_picked_agree_none_p_kernel(
                 in_=z_grouped[:, cols, :].rearrange("p v t -> p (v t)"),
             )
 
-        def cast3(lo, hi, engine):
-            if lo == 0:
-                grouped["w3"] = sb("grp3", [P, 1, N, PACK], BF16, "lg1")
-            g = grouped["w3"][:, :, lo:hi]
-            grouped["w3", lo] = g
-            src = raw3[:, :, lo:hi].rearrange("p j (c i) -> p c j i", i=4)
-            copy_on(engine, g[:, 0].rearrange("p (c i) j -> p c j i", i=4), src)
+        grouped3 = {}
+        codes3 = {}
+        scales3 = sb("scales3", [P, N], U8)
 
-        def last_layer(bank, blocks, first, end, engine):
+        def cast3_last():
+            grouped3[3 * P] = sb("grp3_last", [P, P, PACK], BF16, "rows12")[:]
+            src = raw3[:, :, 3 * P :].rearrange("p j (c i) -> p c j i", i=4)
+            nc.scalar.copy(out=grouped3[3 * P].rearrange("p (c i) j -> p c j i", i=4), in_=src)
+
+        def cast3(lo, hi):
+            if lo == 0:
+                grouped3["all"] = sb("grp3", [P, 3 * P, PACK], BF16, "rows03")
+            grouped3[lo] = grouped3["all"][:, lo:hi]
+            src = raw3[:, :, lo:hi].rearrange("p j c -> p c j")
+            nc.gpsimd.tensor_scalar(out=grouped3[lo], in0=src, scalar1=1.0, scalar2=0.0, op0=MULT, op1=ADD)
+
+        def quant3(lo, hi, tag=None):
+            piece = sb(f"codes3{lo}", [P, hi - lo], U32, tag)
+            for block in range(lo // P, hi // P):
+                codes3[block] = piece[:, block * P - lo : (block + 1) * P - lo]
+            nc.vector.quantize_mx(
+                out=piece[:].bitcast(FP8X4),
+                scales=scales3[:, lo:hi],
+                in_=(grouped3[lo] if lo == 3 * P else grouped3["all"][:, lo:hi]).rearrange("p c j -> p (c j)"),
+            )
+
+        def last_layer(b, blocks, first, end, engine):
             n = len(blocks)
-            acc = psum.tile([P, n, end - first], F32, name=f"out{bank}", tag=f"bank{bank}")
+            acc = bank(f"out{b}", [P, n, end - first], b)
             for i, block in enumerate(blocks):
-                lo = max(start for start, stop in W3_PIECES if start <= block * P)
-                cols = slice(block * P - lo, (block + 1) * P - lo)
+                m = slice(block * P, (block + 1) * P)
                 nc.tensor.matmul_mx(
                     out=acc[:, i, :],
-                    lhsT=codes["w3", lo][:, cols].bitcast(FP8X4),
-                    lhsT_scale=scales["w3", lo][:, cols],
+                    lhsT=codes3[block].bitcast(FP8X4),
+                    lhsT_scale=scales3[:, m],
                     rhs=z_codes[:, first:end].bitcast(FP8X4),
                     rhs_scale=z_scales[:, first:end],
                     start=True,
                     stop=True,
                 )
-            res = sb(f"res{bank}", [P, n, end - first], F32)
+            res = sb(f"res{b}", [P, n, end - first], F32)
             copy_on(engine, res[:], acc[:])
             rows_out = out[blocks[0] * P : (blocks[0] + n) * P, first:end]
             nc.sync.dma_start(out=rows_out.rearrange("(b p) v -> p b v", p=P), in_=res[:])
 
+        gather_words(0, 0, S)
         cast(0, 0, 0, "scalar")
         cast(0, 0, 1, "scalar")
-        quant((0, 0, 0), 2 * P)
         nc.vector.tensor_copy(xs[:], xs_all[:].indirect(offs_sb[:]))
-        nc.vector.tensor_copy(xw[0][:], xw_all[0][:].indirect(offs_sb[:]))
-        quant((0, 0, 1), 2 * P)
-        first_mm(0, 0, 0, 0, S // 2)
-        first_mm(0, 0, 0, S // 2, S)
-        for t in range(1, PACK):
-            first_mm(0, 0, t)
-        nc.vector.tensor_copy(xw[1][:], xw_all[1][:].indirect(offs_sb[:]))
-        late_cast(0, 0, "vector", 0, P)
-        late_cast(0, 1, "scalar", 0, P)
-        for a in range(2):
-            late_cast(1, a, "vector", 0, P // 2)
-            late_cast(1, a, "scalar", P // 2, P)
-        late_quant(0)
+        codes[0, 0, 0] = sb("codes00", [P, 2 * P], U32, "xs_all")[:]
+        quant(0, 0, 0)
+        cast(0, 1, 0, "scalar")
+        cast(0, 1, 1, "vector")
+        quant_late(0)
+        quant(0, 1, 0)
+        for t in range(PACK):
+            for lo in (0, S // 2):
+                first_mm(0, 0, t, lo, lo + S // 2)
         for lo in (0, S // 2):
-            first_mm(0, 1, 0, lo, lo + S // 2)
-            evac(0, 0, lo, lo + S // 2)
+            gather_words(1, lo, lo + S // 2)
+            for t in range(PACK):
+                first_mm(0, 1, t, lo, lo + S // 2)
+        evac(0, 0, "scalar", 0, S // 2)
         for t in range(1, PACK):
-            late_quant(t)
-        for t in range(1, PACK):
-            first_mm(0, 1, t)
-        evac(0, 1)
-        gather_keys(0)
+            evac(0, t, "vector", 0, S // 2)
+        for t in range(PACK):
+            evac(0, t, "scalar" if t < 2 else "vector", S // 2, S)
         cast(1, 0, 0, "scalar")
-        gather_keys(1)
-        cast_both(0, "scalar")
-        evac(0, 2)
-        quant((1, 0, 0), 2 * P)
+        cast(1, 0, 1, "scalar")
+        gather_keys(0)
+        quant(1, 0, 0)
+        first_mm(1, 0, 0, 0, S // 2)
+        first_mm(1, 0, 0, S // 2, S)
+        first_mm(1, 0, 1)
         cast(1, 1, 0, "vector")
-        cast_both(1, "scalar")
-        evac(0, 3)
-        codes[1, 1, 0] = sb("codes110", [P, 2 * P], U32)
-        scales[1, 1, 0] = sb("scales110", [P, 2 * P], U8)
-        late_quant(0, 1)
-        late_quant(1, 1)
-        for z in range(PASSES):
-            first_mm(1, z, 0, 0, S // 2)
-            first_mm(1, z, 0, S // 2, S)
-            first_mm(1, z, 1)
-        gather_key(2, 0)
-        quant_both()
-        add_logits(0)
-        gather_key(2, 1)
-        gather_keys(3)
-        add_logits(2)
-        turned_logits(1, 2)
+        cast(1, 1, 1, "scalar")
+        quant(1, 1, 0, 0, 1)
+        quant(1, 1, 0, 1, 2)
+        gather_keys(1)
+        fetch_key(3, 1, "raw11")
+        for lo in (0, S // 2):
+            first_mm(1, 1, 0, lo, lo + S // 2)
+            evac(1, 0, "scalar", lo, lo + S // 2)
+        first_mm(1, 1, 1)
+        evac(1, 1, "scalar")
+        quant_late(1)
+        turned_logits(0)
         for t in (2, 3):
             first_mm(1, 0, t)
             first_mm(1, 1, t)
-        evac(1, 0, 0, S // 2)
-        evac(1, 0, S // 2, S)
-        evac(1, 1)
+        gather_keys(2)
+        gather_keys(3, (0,))
+        pose_key(3, 1)
+        evac(1, 2, "vector")
+        evac(1, 3, "vector")
+        fetch_on_vector(3)
+        fetch(0)
         sigmoid(0)
-        fetch_votes(1)
-        turned_sigmoid(1)
-        turned_logits(3, 3)
-        turn_back(1)
-        evac(1, 2)
-        sigmoid(2)
-        gather_votes(0, 0, V)
-        evac(1, 3, engine="vector")
-        turned_sigmoid(3)
-        turn_back(3)
-        fetch_votes(3, "agree31")
-        for lo, hi in W3_PIECES:
-            cast3(lo, hi, "scalar")
-        weigh(1, 0, V)
-        gather_votes(2, 0, V)
-        for h in range(2):
-            weigh(3, h * HALF, (h + 1) * HALF)
-        for h in range(2):
-            sum_votes(h)
-        for h in range(2):
-            quant_z(h)
-        for lo, hi in W3_PIECES:
-            quant(("w3", lo), hi - lo)
-        last_layer(6, (0, 1), 0, HALF, "scalar")
-        last_layer(7, (0, 1), HALF, V, "vector")
-        last_layer(0, (2,), 0, V, "scalar")
-        last_layer(1, (3,), 0, V, "vector")
+        fetch(1)
+        for t in range(1, PACK):
+            turned_logits(t)
+            sigmoid(t)
+        for t in (0, 1, 3, 2):
+            turn_back(t)
+        fetch(2, 0, HALF, 0)
+        fetch(2, HALF, V, 1024)
+        for lo in range(0, 3 * P, P):
+            cast3(lo, lo + P)
+        cast3_last()
+        votes = sb("votes", [P, 2, PACK, V], F32)
+        weigh(0)
+        weigh(1)
+        quant3(0, 2 * P)
+        weigh(3)
+        weigh(2, 0, HALF)
+        sum_votes(0)
+        weigh(2, HALF, V)
+        quant_z(0)
+        sum_votes(1)
+        quant_z(1)
+        quant3(2 * P, 3 * P, "fetched30")
+        quant3(3 * P, N, 1024)
+        last_layer(3, (0, 1), 0, HALF, "scalar")
+        last_layer(5, (2,), 0, HALF, "scalar")
+        last_layer(4, (0, 1), HALF, V, "scalar")
+        last_layer(6, (3,), 0, HALF, "vector")
+        last_layer(7, (2, 3), HALF, V, "vector")

from contextlib import ExitStack

import concourse.mybir as mybir
from concourse.masks import make_identity

K, T, S, V, N, H = 1024, 2048, 512, 256, 512, 512
FLOPS = 2 * (2 * K * H * S + H * N * V)

F32 = mybir.dt.float32
BF16 = mybir.dt.bfloat16
I32 = mybir.dt.int32
U32 = mybir.dt.uint32
U16 = mybir.dt.uint16
U8 = mybir.dt.uint8
FP8X4 = mybir.dt.float8_e4m3fn_x4
MULT = mybir.AluOpType.mult
ADD = mybir.AluOpType.add
SIGMOID = mybir.ActivationFunctionType.Sigmoid
COPY = mybir.ActivationFunctionType.Copy

P = 128
PACK = 4
K_PASS = P * PACK
PASSES = K // K_PASS
HALF = V // 2


def tile_picked_agree_none_p_kernel(
    tc, x_words, x_scales, w1, w2, pose, lg1, lg2, w3, offs, p1, p2, out
):
    nc = tc.nc
    with ExitStack() as ctx:
        keep = ctx.enter_context(tc.tile_pool(name="keep", bufs=1))
        shared = ctx.enter_context(tc.tile_pool(name="shared", bufs=1))
        psum = ctx.enter_context(tc.psum_pool(name="psum", bufs=1))

        def sb(name, shape, dtype, tag=None):
            if isinstance(tag, int):
                return shared.tile(shape, dtype, name=name, tag=name, align_bytes=64, offset=tag)
            return keep.tile(shape, dtype, name=name, tag=tag or name, align_bytes=64)

        def bank(name, shape, b):
            return psum.tile(shape, F32, name=name, tag=f"bank{b}")

        offs_sb = sb("offs_sb", [P, S // 16], U16)
        lists = [sb("p1_sb", [P, V // 16], U16), sb("p2_sb", [P, V // 16], U16)]
        xs_all = sb("xs_all", [P, T], U8)
        xw_all = [sb(f"xw_all{z}", [P, T], U32) for z in range(PASSES)]
        xs = sb("xs", [P, S], U8)
        xw = [sb(f"xw{z}", [P, S], U32) for z in range(PASSES)]
        raw = {(w, z): sb(f"raw{w}{z}", [P, PACK, H], F32) for w in range(2) for z in range(PASSES)}
        raw3 = sb("raw3", [P, PACK, N], F32)
        pose_parts = {lo: sb(f"pose{lo}", [P, hi - lo, V], F32) for lo, hi in ((0, 1), (1, 3), (3, 4))}
        pose_of = [pose_parts[0][:, 0:1], pose_parts[1][:, 0:1], pose_parts[1][:, 1:2], pose_parts[3][:, 0:1]]
        lg_sb = [sb(f"lg{a}", [P, 2, 2, V], F32) for a in range(2)]
        warm = sb("warm", [P, 1], F32)
        ident = sb("ident", [P, P], F32)
        make_identity(nc, ident[:])

        def load_rows(dst, src, z):
            nc.sync.dma_start(out=dst[:], in_=src[z * K_PASS : (z + 1) * K_PASS, :].rearrange("(p j) c -> p j c", j=PACK))

        def load_words(z, lo=0, hi=T):
            nc.sync.dma_start(
                out=xw_all[z][:, lo:hi].bitcast(I32),
                in_=x_words[z].rearrange("p n r -> p (n r)").bitcast(I32)[:, lo:hi],
            )

        def load_pair(dst, src, a):
            nc.sync.dma_start(out=dst, in_=src.rearrange("(p t) v -> p t v", t=PACK)[:, 2 * a : 2 * a + 2, :])

        def load_poses(lo, hi):
            nc.sync.dma_start(out=pose_parts[lo][:], in_=pose.rearrange("(p t) v -> p t v", t=PACK)[:, lo:hi, :])

        def load_scales(h):
            for r in (2 * h, 2 * h + 1):
                for z in range(PASSES):
                    nc.sync.dma_start(
                        out=xs_all[4 * z + r : P : 32, :].bitcast(I32),
                        in_=x_scales[z, r : 16 : 4, :].bitcast(I32),
                    )

        def load_logits(a):
            load_pair(lg_sb[a][:, 0], lg1, a)
            load_pair(lg_sb[a][:, 1], lg2, a)

        nc.vector.memset(xs_all[:].bitcast(I32), 0)
        nc.vector.memset(warm[:], 0.0)
        nc.scalar.activation(out=warm[:], in_=warm[:], func=SIGMOID)
        load_words(0, 0, T // 2)
        nc.sync.dma_start(offs_sb[:], offs)
        load_scales(0)
        load_words(0, T // 2, T)
        load_rows(raw[0, 0], w1, 0)
        load_scales(1)
        load_rows(raw[0, 1], w1, 1)
        load_words(1)
        load_rows(raw[1, 0], w2, 0)
        nc.sync.dma_start(lists[0][:], p1)
        load_poses(0, 1)
        nc.sync.dma_start(lists[1][:], p2)
        load_rows(raw[1, 1], w2, 1)
        load_poses(1, 3)
        load_poses(3, 4)
        load_pair(lg_sb[0][:, 0], lg1, 0)
        load_pair(lg_sb[0][:, 1], lg2, 0)
        load_rows(raw3, w3, 0)
        load_logits(1)

        keys = [(w, z) for w in range(2) for z in range(PASSES)]
        grouped = {(w, z, 0): sb(f"grp{w}{z}", [P, 2, P, PACK], BF16)[:] for w, z in keys}
        codes = {(w, z, 0): sb(f"codes{w}{z}", [P, 2 * P], U32)[:] for w, z in keys[1:]}
        scales = {(w, z, 0): sb(f"scales{w}{z}", [P, 2 * P], U8)[:] for w, z in keys}
        late = [sb(f"late{w}", [P, PASSES, 2, P, PACK], BF16) for w in range(2)]
        late_codes = [sb(f"late_codes{w}", [P, PASSES, 2 * P], U32) for w in range(2)]
        late_scales = [sb(f"late_scales{w}", [P, PASSES, 2 * P], U8) for w in range(2)]
        for w, z in keys:
            grouped[w, z, 1] = late[w][:, z]
            codes[w, z, 1] = late_codes[w][:, z]
            scales[w, z, 1] = late_scales[w][:, z]

        def quant_late(w):
            nc.vector.quantize_mx(
                out=late_codes[w][:].rearrange("p z c -> p (z c)").bitcast(FP8X4),
                scales=late_scales[w][:].rearrange("p z c -> p (z c)"),
                in_=late[w][:].rearrange("p z b m j -> p (z b m j)"),
            )

        def copy_on(engine, out_ap, in_ap):
            if engine == "vector":
                nc.vector.tensor_copy(out=out_ap, in_=in_ap)
            else:
                nc.scalar.copy(out=out_ap, in_=in_ap)

        def cast(w, z, a, engine, lo=0, hi=P):
            src = raw[w, z][:].rearrange("p j (m a b) -> p a m j b", a=2, b=2)[:, a, lo:hi]
            copy_on(engine, grouped[w, z, a][:, :, lo:hi].rearrange("p b m j -> p m j b"), src)

        def quant(w, z, a, b0=0, b1=2):
            cols = slice(b0 * P, b1 * P)
            nc.vector.quantize_mx(
                out=codes[w, z, a][:, cols].bitcast(FP8X4),
                scales=scales[w, z, a][:, cols],
                in_=grouped[w, z, a][:, b0:b1].rearrange("p b m j -> p (b m j)"),
            )

        def gather_words(z, lo, hi):
            nc.vector.tensor_copy(xw[z][:, lo:hi], xw_all[z][:].indirect(offs_sb[:, lo // 16 : hi // 16]))

        banks = {}
        bank_of = {(0, t, h * S // 2): PACK * h + t for t in range(PACK) for h in range(2)}
        bank_of.update({(1, 0, 0): 0, (1, 0, S // 2): 1, (1, 1, 0): 2, (1, 2, 0): 3, (1, 3, 0): 4})

        def first_mm(w, z, t, lo=0, hi=S):
            if z == 0:
                banks[w, t, lo] = bank(f"acc{w}{t}{lo}", [P, hi - lo], bank_of[w, t, lo])
            key, cols = (w, z, t // 2), slice(P * (t % 2), P * (t % 2 + 1))
            nc.tensor.matmul_mx(
                out=banks[w, t, lo][:],
                lhsT=codes[key][:, cols].bitcast(FP8X4),
                lhsT_scale=scales[key][:, cols],
                rhs=xw[z][:, lo:hi].bitcast(FP8X4),
                rhs_scale=xs[4 * z : P, lo:hi],
                start=(z == 0),
                stop=(z == PASSES - 1),
            )

        rows = {(w, t): sb(f"rows{w}{t}", [P, S], F32) for w in range(2) for t in range(PACK)}

        def evac(w, t, engine, lo=0, hi=S):
            copy_on(engine, rows[w, t][:, lo:hi], banks[w, t, lo][:])

        agree = [sb(f"agree{t}", [P, 2, V], F32) for t in range(PACK - 1)] + [sb("agree3", [P, 2, V], F32, 0)]
        gate = [sb(f"gate{t}", [P, 2, V], F32) for t in range(PACK)]

        plain_keys = {}

        def gather_keys(t, children=(0, 1)):
            for l in children:
                nc.vector.tensor_tensor(
                    agree[t][:, l, :], rows[0, t][:].indirect(lists[l][:]), pose_of[t][:, 0, :], MULT
                )

        def fetch_key(t, l, tag):
            plain_keys[t, l] = sb(f"plain_key{t}{l}", [P, V], F32, tag)
            nc.scalar.activation(out=plain_keys[t, l][:], in_=rows[0, t][:].indirect(lists[l][:]), func=COPY)

        def pose_key(t, l):
            nc.vector.tensor_tensor(agree[t][:, l, :], plain_keys[t, l][:], pose_of[t][:, 0, :], MULT)

        logit, gate_bank, fetched = {}, {}, {}
        logit_bank = (0, 1, 2, 5)
        back_bank = (6, 7, 1, 0)

        def turn(dst, src, start, stop):
            nc.tensor.matmul(dst, lhsT=src, rhs=ident[:], start=start, stop=stop, is_transpose=True)

        def turned_logits(t):
            logit[t] = bank(f"logit{t}", [P, 2, V], logit_bank[t])
            for l in range(2):
                for h in range(2):
                    cols = slice(h * HALF, (h + 1) * HALF)
                    turn(logit[t][:, l, cols], lg_sb[t // 2][:, l, t % 2, cols], True, False)
                    turn(logit[t][:, l, cols], agree[t][:, l, cols], False, True)

        def sigmoid(t):
            nc.scalar.activation(out=gate[t][:], in_=logit[t][:], func=SIGMOID)

        def turn_back(t):
            gate_bank[t] = bank(f"gateb{t}", [P, 2, V], back_bank[t])
            for h in range(2):
                for l in range(2):
                    cols = slice(h * HALF, (h + 1) * HALF)
                    turn(gate_bank[t][:, l, cols], gate[t][:, l, cols], True, True)

        def fetch(t, lo=0, hi=V, tag=None, children=(0, 1)):
            fetched[t, lo] = sb(f"fetched{t}{lo}", [P, 2, hi - lo], F32, tag)
            for l in children:
                nc.scalar.activation(
                    out=fetched[t, lo][:, l, :],
                    in_=rows[1, t][:].indirect(lists[l][:, lo // 16 : hi // 16]),
                    func=COPY,
                )

        def fetch_on_vector(t):
            fetched[t, 0] = sb(f"fetched{t}0", [P, 2, V], F32)
            for l in range(2):
                nc.vector.tensor_copy(fetched[t, 0][:, l, :], rows[1, t][:].indirect(lists[l][:]))

        def add_logits(t):
            nc.vector.tensor_tensor(agree[t][:], agree[t][:], lg_sb[t // 2][:, :, t % 2, :], ADD)

        def plain_sigmoid(t):
            nc.scalar.activation(out=gate[t][:], in_=agree[t][:], func=SIGMOID)

        def gather_votes(t, lo=0, hi=V, children=(0, 1)):
            for l in children:
                nc.vector.tensor_tensor(
                    votes[:, l, t, lo:hi],
                    rows[1, t][:].indirect(lists[l][:, lo // 16 : hi // 16]),
                    gate[t][:, l, lo:hi],
                    MULT,
                )

        def weigh(t, lo=0, hi=V):
            nc.vector.tensor_tensor(votes[:, :, t, lo:hi], fetched[t, lo][:], gate_bank[t][:, :, lo:hi], MULT)

        z_grouped = sb("z_grouped", [P, V, PACK], BF16)
        z_codes = sb("z_codes", [P, V], U32)
        z_scales = sb("z_scales", [P, V], U8)

        def sum_votes(h):
            cols = slice(h * HALF, (h + 1) * HALF)
            walk = "p t (c i) -> p c t i"
            nc.vector.tensor_tensor(
                z_grouped[:, cols, :].rearrange("p (c i) t -> p c t i", i=4),
                votes[:, 0, :, cols].rearrange(walk, i=4),
                votes[:, 1, :, cols].rearrange(walk, i=4),
                ADD,
            )

        def quant_z(h):
            cols = slice(h * HALF, (h + 1) * HALF)
            nc.vector.quantize_mx(
                out=z_codes[:, cols].bitcast(FP8X4),
                scales=z_scales[:, cols],
                in_=z_grouped[:, cols, :].rearrange("p v t -> p (v t)"),
            )

        grouped3 = {}
        codes3 = {}
        scales3 = sb("scales3", [P, N], U8)

        def cast3_last():
            grouped3[3 * P] = sb("grp3_last", [P, P, PACK], BF16, "rows12")[:]
            src = raw3[:, :, 3 * P :].rearrange("p j (c i) -> p c j i", i=4)
            nc.scalar.copy(out=grouped3[3 * P].rearrange("p (c i) j -> p c j i", i=4), in_=src)

        def cast3(lo, hi):
            if lo == 0:
                grouped3["all"] = sb("grp3", [P, 3 * P, PACK], BF16, "rows03")
            grouped3[lo] = grouped3["all"][:, lo:hi]
            src = raw3[:, :, lo:hi].rearrange("p j c -> p c j")
            nc.gpsimd.tensor_scalar(out=grouped3[lo], in0=src, scalar1=1.0, scalar2=0.0, op0=MULT, op1=ADD)

        def quant3(lo, hi, tag=None):
            piece = sb(f"codes3{lo}", [P, hi - lo], U32, tag)
            for block in range(lo // P, hi // P):
                codes3[block] = piece[:, block * P - lo : (block + 1) * P - lo]
            nc.vector.quantize_mx(
                out=piece[:].bitcast(FP8X4),
                scales=scales3[:, lo:hi],
                in_=(grouped3[lo] if lo == 3 * P else grouped3["all"][:, lo:hi]).rearrange("p c j -> p (c j)"),
            )

        def last_layer(b, blocks, first, end, engine):
            n = len(blocks)
            acc = bank(f"out{b}", [P, n, end - first], b)
            for i, block in enumerate(blocks):
                m = slice(block * P, (block + 1) * P)
                nc.tensor.matmul_mx(
                    out=acc[:, i, :],
                    lhsT=codes3[block].bitcast(FP8X4),
                    lhsT_scale=scales3[:, m],
                    rhs=z_codes[:, first:end].bitcast(FP8X4),
                    rhs_scale=z_scales[:, first:end],
                    start=True,
                    stop=True,
                )
            res = sb(f"res{b}", [P, n, end - first], F32)
            copy_on(engine, res[:], acc[:])
            rows_out = out[blocks[0] * P : (blocks[0] + n) * P, first:end]
            nc.sync.dma_start(out=rows_out.rearrange("(b p) v -> p b v", p=P), in_=res[:])

        gather_words(0, 0, S)
        cast(0, 0, 0, "scalar")
        cast(0, 0, 1, "scalar")
        nc.vector.tensor_copy(xs[:], xs_all[:].indirect(offs_sb[:]))
        codes[0, 0, 0] = sb("codes00", [P, 2 * P], U32, "xs_all")[:]
        quant(0, 0, 0)
        cast(0, 1, 0, "scalar")
        cast(0, 1, 1, "vector")
        quant_late(0)
        quant(0, 1, 0)
        for t in range(PACK):
            for lo in (0, S // 2):
                first_mm(0, 0, t, lo, lo + S // 2)
        for lo in (0, S // 2):
            gather_words(1, lo, lo + S // 2)
            for t in range(PACK):
                first_mm(0, 1, t, lo, lo + S // 2)
        evac(0, 0, "scalar", 0, S // 2)
        for t in range(1, PACK):
            evac(0, t, "vector", 0, S // 2)
        for t in range(PACK):
            evac(0, t, "scalar" if t < 2 else "vector", S // 2, S)
        cast(1, 0, 0, "scalar")
        cast(1, 0, 1, "scalar")
        gather_keys(0)
        quant(1, 0, 0)
        first_mm(1, 0, 0, 0, S // 2)
        first_mm(1, 0, 0, S // 2, S)
        first_mm(1, 0, 1)
        cast(1, 1, 0, "vector")
        cast(1, 1, 1, "scalar")
        quant(1, 1, 0, 0, 1)
        quant(1, 1, 0, 1, 2)
        gather_keys(1)
        fetch_key(3, 1, "raw11")
        for lo in (0, S // 2):
            first_mm(1, 1, 0, lo, lo + S // 2)
            evac(1, 0, "scalar", lo, lo + S // 2)
        first_mm(1, 1, 1)
        evac(1, 1, "scalar")
        quant_late(1)
        turned_logits(0)
        for t in (2, 3):
            first_mm(1, 0, t)
            first_mm(1, 1, t)
        gather_keys(2)
        gather_keys(3, (0,))
        pose_key(3, 1)
        evac(1, 2, "vector")
        evac(1, 3, "vector")
        fetch_on_vector(3)
        fetch(0)
        sigmoid(0)
        fetch(1)
        for t in range(1, PACK):
            turned_logits(t)
            sigmoid(t)
        for t in (0, 1, 3, 2):
            turn_back(t)
        fetch(2, 0, HALF, 0)
        fetch(2, HALF, V, 1024)
        for lo in range(0, 3 * P, P):
            cast3(lo, lo + P)
        cast3_last()
        votes = sb("votes", [P, 2, PACK, V], F32)
        weigh(0)
        weigh(1)
        quant3(0, 2 * P)
        weigh(3)
        weigh(2, 0, HALF)
        sum_votes(0)
        weigh(2, HALF, V)
        quant_z(0)
        sum_votes(1)
        quant_z(1)
        quant3(2 * P, 3 * P, "fetched30")
        quant3(3 * P, N, 1024)
        last_layer(3, (0, 1), 0, HALF, "scalar")
        last_layer(5, (2,), 0, HALF, "scalar")
        last_layer(4, (0, 1), HALF, V, "scalar")
        last_layer(6, (3,), 0, HALF, "vector")
        last_layer(7, (2, 3), HALF, V, "vector")
